import numpy as np, ml_dtypes
CORES = [36,164,52,180,100,228,116,244]
N = 8
import mx_ref
BF = ml_dtypes.bfloat16
def cols(t, e):
    v = np.concatenate([t.reshape(128, -1, 4), np.zeros((128, 1, 4), BF)], axis=1)
    return np.ascontiguousarray(v[:, e]).reshape(128, -1)
def f(rng, *shape):
    return mx_ref.flush((rng.standard_normal(shape, dtype=np.float32) * np.exp2(rng.integers(-2, 3, shape[:-1] + (1,)))).astype(BF))
def wide(rng, *shape, cols=0):
    v = rng.standard_normal(shape, dtype=np.float32) * np.exp2(rng.integers(-12, 13, shape)).astype(np.float32)
    if cols: v *= np.repeat(np.exp2(rng.integers(-cols, cols + 1, shape[:-2] + (1, shape[-1] // 4))) * (rng.random(shape[:-2] + (1, shape[-1] // 4)) > 0.0625), 4, axis=-1).astype(np.float32)
    return mx_ref.flush(v.astype(BF))
T, K, O = 256, 128, 2
def setup_inputs(rng):
    u = np.zeros((128, 512), BF); u[:, :4] = f(rng, 128, 4)
    return {"x": f(rng, N, 128, 4 * T), "u": np.stack([u] * N), "w": f(rng, N, 128, 512 * O)}
def signs(d):
    return np.where(d["u"][0][:, :4].astype(np.float32) < 0, -1, 1).astype(np.float32)
def blocks(rng, n):
    return np.repeat(rng.permutation(16) < n, 8)
def plant(rng, d, n):
    for s in range(N):
        v = d["x"][s].astype(np.float32).reshape(128, T, 4)
        k = rng.permutation(T)[:n[s]]
        v[:, k] = np.abs(v[:, k]) * signs(d)[:, None] * np.float32(8)
        d["x"][s] = v.reshape(128, -1).astype(BF)
    return d
def setup_inputs_one(rng):
    d = setup_inputs(rng); return plant(rng, d, np.where(np.arange(N) == rng.integers(0, N), K, 0))
def setup_inputs_zeros(rng):
    d = setup_inputs(rng); m = blocks(rng, 2)
    d["u"][:, ~m] = 0
    k = rng.permutation(N * T); g = np.full(N * T, -1, np.float32)
    g[k[:K // 3]] = 1; g[k[K // 3:2 * (K // 3)]] = 0
    v = np.abs(d["x"][:, m].astype(np.float32)).reshape(N, -1, T, 4)
    d["x"][:, m] = (v * signs(d)[m][:, None] * g.reshape(N, 1, T, 1)).reshape(N, -1, 4 * T).astype(BF)
    return d
def setup_inputs_few(rng):
    d = setup_inputs(rng); p = rng.permutation(N); g = p[N - N // 2:]
    d["x"][g] = (-np.abs(d["x"][g].astype(np.float32)) * np.tile(signs(d), (1, T))).astype(BF)
    n = np.zeros(N, int); n[p[:2]] = [K * 3 // 5, K - K * 3 // 5]
    return plant(rng, d, n)
def setup_inputs_ties(rng):
    d = setup_inputs(rng); b = f(rng, 128, 4 * 40); m = blocks(rng, 4)
    d["u"][:, m] = 0
    d["x"] = np.stack([cols(b, rng.permutation(np.arange(T) % 40)) for r in range(N)])
    d["x"][:, m] = f(rng, N, 32, 4 * T); return d
def setup_inputs_spread(rng):
    d = setup_inputs(rng); d["x"] = wide(rng, N, 128, 4 * T, cols=8); return d
def check_inputs(d):
    b = []
    u = d["u"].astype(np.float32)
    if (u != u[:1]).any(): b.append("u_same")
    if (u[:, :, 4:] != 0).any(): b.append("u_zero")
    return b
def reference(x, u, w):
    s = np.stack([mx_ref.matmul(mx_ref.quantize(u[r]), mx_ref.quantize(x[r]))[0] for r in range(N)]).reshape(-1) + np.float32(0.0)
    best = np.lexsort((np.arange(N * T), -s))[:K]
    V = mx_ref.quantize(cols(np.concatenate(list(x), axis=1), best))
    y = np.zeros((N, 128, O * K), np.float32)
    for r in range(N):
        for o in range(O): y[r][:, K * o:K * o + K] = mx_ref.matmul(mx_ref.quantize(np.ascontiguousarray(w[r][:, 512 * o:512 * o + 512])), V)
    who = np.stack([best // T, best % T]).astype(np.float32)
    return {"y": y, "id": np.stack([who] * N)}

@@ -1,0 +1,292 @@
+from concourse.mybir import dt, AluOpType, AxisListType, ActivationFunctionType
+
+N, T_COLS, K, O = 8, 256, 128, 2
+BF, F32, U16, I32, CODE, U8 = "bfloat16", "float32", "uint16", "int32", "float8_e4m3fn_x4", "uint8"
+PITCH = 144
+
+SCRATCH = {
+    "UT": ("sbuf", [128, 512], BF), "UQ0": ("sbuf", [128, 128], CODE), "US0": ("sbuf", [128, 128], U8),
+    "UQ": ("sbuf", [128, 128], CODE), "US": ("sbuf", [128, 128], U8), "UOFF": ("sbuf", [128, 8], U16),
+    "XT": ("sbuf", [128, 1024], BF), "XQ": ("sbuf", [128, 256], CODE), "XS": ("sbuf", [128, 256], U8),
+    "WT": ("sbuf", [128, 1024], BF), "WQ": ("sbuf", [128, 256], CODE), "WS": ("sbuf", [128, 256], U8),
+    "PIDX": ("sbuf", [128, 1], I32), "MI": ("sbuf", [128, 1], I32), "MF": ("sbuf", [128, 1], F32), "PF": ("sbuf", [128, 1], F32),
+    "TMOD": ("sbuf", [128, 256], BF), "MASK": ("sbuf", [128, 256], BF), "HOLD": ("sbuf", [128, 256], BF),
+    "J256": ("sbuf", [128, 256], BF), "JC": ("sbuf", [128, 256], BF), "KI": ("sbuf", [128, 128], F32),
+    "KMF": ("sbuf", [128, 128], F32), "KM": ("sbuf", [128, 128], BF), "I16": ("sbuf", [128, 8], F32),
+    "TRI": ("sbuf", [128, 128], BF), "ZB": ("sbuf", [128, 128], BF),
+    "CH0": ("sbuf", [128, 384], BF), "CH1": ("sbuf", [128, 384], BF), "EQ0": ("sbuf", [128, 128], BF), "EQ1": ("sbuf", [128, 128], BF),
+    "LR": ("sbuf", [128, 2], F32), "BX": ("sbuf", [128, 64], BF), "TR": ("sbuf", [128, 64], BF), "LRF": ("sbuf", [128, 256], BF),
+    "LX": ("sbuf", [128, 256], BF), "LH": ("sbuf", [128, 256], BF), "LU": ("sbuf", [128, 16], U16), "INV": ("sbuf", [128, 256], BF),
+    "IX": ("sbuf", [128, 128], BF), "IH": ("sbuf", [128, 128], BF), "LO0": ("sbuf", [128, 8], U16),
+    "AX": ("sbuf", [128, 128], F32), "A16": ("sbuf", [128, 128], F32), "CMP": ("sbuf", [128, 8 * PITCH], BF),
+    "PA": ("sbuf", [128, 8], F32), "PAU": ("sbuf", [128, 8], U16), "TS": ("sbuf", [128, 128], BF), "EB": ("sbuf", [128, 128], BF),
+    "P1": ("sbuf", [128, 128], BF), "UU": ("sbuf", [128, 128], BF), "MX": ("sbuf", [128, 128], BF), "MH": ("sbuf", [128, 128], BF),
+    "NX": ("sbuf", [128, 256], BF), "NH": ("sbuf", [128, 256], BF),
+    "RES0": ("sbuf", [128, 256], F32), "RES1": ("sbuf", [128, 256], F32), "YB": ("sbuf", [128, 256], F32), "IDB": ("sbuf", [128, 256], F32),
+    "BSF": ("psum", [128, 512], F32), "BS0": ("psum", [128, 512], F32), "BS1": ("psum", [128, 512], F32), "BA": ("psum", [128, 512], F32),
+    "BB": ("psum", [128, 512], F32), "BY0": ("psum", [128, 512], F32), "BY1": ("psum", [128, 512], F32),
+}
+for _h in (1, 2, 3):
+    SCRATCH["W%dQ" % _h] = ("sbuf", [128, 256], CODE)
+    SCRATCH["W%dS" % _h] = ("sbuf", [128, 256], U8)
+    SCRATCH["E%d" % _h] = ("sbuf", [128, 256], BF)
+    SCRATCH["LO%d" % _h] = ("sbuf", [128, 8], U16)
+    SCRATCH["R%d" % _h] = ("sbuf", [128, 256], BF)
+    SCRATCH["C%d" % _h] = ("sbuf", [128, 256], BF)
+    SCRATCH["NS%d" % _h] = ("sbuf", [128, 16], U16)
+    SCRATCH["NL%d" % _h] = ("sbuf", [128, 16], U16)
+
+PSUM_NAMES = [n for n in SCRATCH if SCRATCH[n][0] == "psum"]
+SEMAPHORES = ["v", "s", "t", "gc", "du", "dx0", "dx1", "dw0", "dw1", "dy0", "dy1", "did", "loc",
+              "arr1", "arr2", "arr3", "num1", "num2", "num3"]
+
+
+def rank_program(g, core, T, topo):
+    rank = T.rank_of(core)
+    if rank is None:
+        return
+    A = AluOpType
+    F = ActivationFunctionType
+    engines = {"v": g.vector, "s": g.scalar, "t": g.tensor, "g": g, "y": g.sync}
+    known = {q: {} for q in engines}
+    total = {}
+    hist = {}
+
+    def record(reads, writes, q, sem, val, clock):
+        for rs, w in ((reads, False), (writes, True)):
+            for r in rs:
+                hist.setdefault(r[0], []).append((r[1], r[2], w, q, sem, val, clock))
+
+    def hold(q, reads, writes):
+        need = {}
+        for rs, w in ((reads, False), (writes, True)):
+            for r in rs:
+                psum = r[0] in PSUM_NAMES
+                for lo, hi, hw, hq, sem, val, clock in hist.get(r[0], []):
+                    if not (psum or (lo < r[2] and r[1] < hi)):
+                        continue
+                    if not (w or hw or (psum and hq != q)):
+                        continue
+                    if known[q].get(sem, 0) < val and (sem not in need or need[sem][0] < val):
+                        need[sem] = (val, clock)
+        for sem in sorted(need):
+            val, clock = need[sem]
+            if any(o != sem and need[o][1].get(sem, 0) >= val for o in need):
+                continue
+            engines[q].wait_ge(T.sem[sem], val)
+        for sem in need:
+            val, clock = need[sem]
+            for s, x in list(clock.items()) + [(sem, val)]:
+                known[q][s] = max(known[q].get(s, 0), x)
+
+    def do(q, call, writes, reads, sem=None, inc=1):
+        sem = sem or {"g": "gc"}.get(q, q)
+        hold(q, reads, writes)
+        call().then_inc(T.sem[sem], inc)
+        total[sem] = total.get(sem, 0) + inc
+        clock = dict(known[q])
+        clock[sem] = total[sem]
+        record(reads, writes, q, sem, total[sem], clock)
+
+    def ap(r):
+        return T[r[0]][:, r[1]:r[2]] if len(r) == 3 else T[r[0]][:, r[1]:r[2]:r[3]]
+
+    def words(r):
+        return ap(r).bitcast(dt.uint32)
+
+    def ts(out, in0, s, op):
+        col = isinstance(s, tuple)
+        do("v", lambda: g.vector.tensor_scalar(ap(out), ap(in0), ap(s) if col else s, None, op), [out], [in0, s] if col else [in0])
+
+    def tt(out, a, b, op):
+        do("v", lambda: g.vector.tensor_tensor(ap(out), ap(a), ap(b), op), [out], [a, b])
+
+    def scan(out, a, b, init, op0, op1):
+        do("v", lambda: g.vector.tensor_tensor_scan(ap(out), ap(a), ap(b), init, op0, op1), [out], [a, b])
+
+    def copy(out, a):
+        do("v", lambda: g.vector.tensor_copy(ap(out), ap(a)), [out], [a])
+
+    def scopy(out, a):
+        do("s", lambda: g.scalar.activation(ap(out), ap(a), F.Copy), [out], [a])
+
+    def vpick(out, win, off):
+        do("v", lambda: g.vector.tensor_copy(ap(out), ap(win).indirect(ap(off))), [out], [win, off])
+
+    def spick(out, win, off):
+        do("s", lambda: g.scalar.activation(ap(out), ap(win).indirect(ap(off)), F.Copy), [out], [win, off])
+
+    def pick_columns(q2, s2, q1, s1, off):
+        do("v", lambda: g.vector.tensor_copy(words(q2), words(q1).indirect(ap(off))), [q2], [q1, off])
+        spick(s2, s1, off)
+
+    def fill(out, x):
+        do("v", lambda: g.vector.memset(ap(out), x), [out], [])
+
+    def iota(out, pattern, base, cm):
+        do("g", lambda: g.iota(ap(out), pattern, base, cm, allow_small_or_imprecise_dtypes=True), [out], [])
+
+    def quant(q, s, t):
+        do("v", lambda: g.vector.quantize_mx(ap(q), ap(s), ap(t)), [q, s], [t])
+
+    def mm(out, wq, ws, xq, xs):
+        do("t", lambda: g.tensor.matmul_mx(ap(out), ap(wq), ap(ws), ap(xq), ap(xs), True, True), [out], [wq, ws, xq, xs])
+
+    def accum(buf, out):
+        do("s", lambda: g.scalar.activation(ap(buf), ap(buf), F.Identity, accum_out=ap(out)), [buf, out], [buf])
+
+    def load(q, out, src, sem):
+        do(q, lambda: engines[q].dma_start(ap(out), src), [out], [], sem, 16)
+
+    def send(dst, out, src, rsem, codes=False):
+        hold("g", [src], [])
+        rid, pid = topo.addr(dst, core)
+        a, b = (ap(out).bitcast(dt.uint8), ap(src).bitcast(dt.uint8)) if codes else (ap(out), ap(src))
+        g.remote_dma(a, b, T.sem[rsem], T.sem["loc"], pid, rid, topo.mask(core, dst))
+        n = len(topo.engines(core, dst))
+        total["loc"] = total.get("loc", 0) + n
+        total[rsem] = total.get(rsem, 0) + n
+
+    def arrive(regions, sem):
+        record([], regions, "-", sem, total[sem], {sem: total[sem]})
+
+    load("y", ("UT", 0, 8), T.u[:, 0:8], "du")
+    load("s", ("XT", 0, 512), T.x[:, 0:512], "dx0")
+    load("y", ("XT", 512, 1024), T.x[:, 512:1024], "dx1")
+
+    fill(("UT", 8, 512), 0.0)
+    fill(("UOFF", 0, 8), 0)
+    fill(("ZB", 0, 128), 0.0)
+    iota(("PIDX", 0, 1), [[0, 1]], 0, 1)
+    iota(("TMOD", 0, 256), [[0, 16], [1, 16]], 0, 0)
+    iota(("J256", 0, 256), [[1, 256]], 0, 0)
+    iota(("JC", 0, 256), [[32, 4], [128, 2], [1, 32]], 0, 0)
+    iota(("I16", 0, 8), [[16, 8]], 0, 0)
+    iota(("KI", 0, 128), [[1, 128]], 127 + 4096, 0)
+    do("v", lambda: g.vector.tensor_scalar(ap(("MI", 0, 1)), ap(("PIDX", 0, 1)), 15, None, A.bitwise_and), [("MI", 0, 1)], [("PIDX", 0, 1)])
+    copy(("MF", 0, 1), ("MI", 0, 1))
+    copy(("PF", 0, 1), ("PIDX", 0, 1))
+    ts(("MASK", 0, 256), ("TMOD", 0, 256), ("MF", 0, 1), A.is_equal)
+    ts(("HOLD", 0, 256), ("TMOD", 0, 256), ("MF", 0, 1), A.is_gt)
+    ts(("TRI", 0, 128), ("J256", 0, 128), ("PF", 0, 1), A.is_lt)
+
+    quant(("UQ0", 0, 128), ("US0", 0, 128), ("UT", 0, 512))
+    pick_columns(("UQ", 0, 128), ("US", 0, 128), ("UQ0", 0, 128), ("US0", 0, 128), ("UOFF", 0, 8))
+    U = (("UQ", 0, 128), ("US", 0, 128))
+    for h in (0, 1):
+        quant(("XQ", 128 * h, 128 * h + 128), ("XS", 128 * h, 128 * h + 128), ("XT", 512 * h, 512 * h + 512))
+    mm(("BS0", 0, 128), ("XQ", 0, 128), ("XS", 0, 128), *U)
+    mm(("BSF", 0, 256), *U, ("XQ", 0, 256), ("XS", 0, 256))
+    mm(("BS1", 0, 128), ("XQ", 128, 256), ("XS", 128, 256), *U)
+
+    s0, s1 = ("BS0", 0, 1), ("BS1", 0, 1)
+    ts(("EQ0", 0, 128), ("BSF", 0, 128), s0, A.is_equal)
+    ts(("CH0", 0, 256), ("BSF", 0, 256), s0, A.is_gt)
+    tt(("CH0", 256, 384), ("EQ0", 0, 128), ("TRI", 0, 128), A.mult)
+    accum(("CH0", 0, 384), ("LR", 0, 1))
+    ts(("EQ1", 0, 128), ("BSF", 128, 256), s1, A.is_equal)
+    ts(("CH1", 0, 128), ("BSF", 0, 128), s1, A.is_ge)
+    ts(("CH1", 128, 256), ("BSF", 128, 256), s1, A.is_gt)
+    tt(("CH1", 256, 384), ("EQ1", 0, 128), ("TRI", 0, 128), A.mult)
+    accum(("CH1", 0, 384), ("LR", 1, 2))
+    for h in (0, 1):
+        ts(("BX", 32 * h, 32 * h + 32), ("ZB", 0, 32), ("LR", h, h + 1), A.add)
+    do("v", lambda: g.vector.transpose(ap(("TR", 0, 64)), ap(("BX", 0, 64))), [("TR", 0, 64)], [("BX", 0, 64)])
+    for a in range(4):
+        out = ("LRF", 64 * a, 64 * a + 64)
+        do("g", lambda: g.partition_broadcast(ap(out), T.TR[32 * a:32 * a + 1, 0:64], 128), [out], [("TR", 0, 64)])
+    tt(("LX", 0, 256), ("LRF", 0, 256), ("MASK", 0, 256), A.mult)
+    scan(("LH", 0, 256), ("HOLD", 0, 256), ("LX", 0, 256), 0.0, A.mult, A.add)
+    copy(("LU", 0, 16), ("LH", 15, 256, 16))
+    do("v", lambda: g.vector.tensor_copy(T.INV[:, 0:256].indirect(T.LU[:, 0:16]), T.JC[:, 0:256]),
+       [("INV", 0, 256)], [("LU", 0, 16), ("JC", 0, 256)])
+    tt(("IX", 0, 128), ("INV", 0, 128), ("MASK", 0, 128), A.mult)
+    scan(("IH", 0, 128), ("HOLD", 0, 128), ("IX", 0, 128), 0.0, A.mult, A.add)
+    copy(("LO0", 0, 8), ("IH", 15, 128, 16))
+    pick_columns(("W1Q", 0, 128), ("W1S", 0, 128), ("XQ", 0, 256), ("XS", 0, 256), ("LO0", 0, 8))
+
+    for h in (1, 2, 3):
+        wq, ws, n, c, r = "W%dQ" % h, "W%dS" % h, "NL%d" % h, "C%d" % h, "R%d" % h
+        own, got = ((wq, 0, 128), (ws, 0, 128)), ((wq, 128, 256), (ws, 128, 256))
+        bit = 1 << (h - 1)
+        mate = rank ^ bit
+        dst = T.cores[mate]
+        send(dst, got[0], own[0], "arr%d" % h, codes=True)
+        send(dst, got[1], own[1], "arr%d" % h)
+        arrive(got, "arr%d" % h)
+        mm(("BA", 0, 128), *U, *own)
+        tt(("AX", 0, 128), ("BA", 0, 128), ("MASK", 0, 128), A.mult)
+        scan(("A16", 0, 128), ("HOLD", 0, 128), ("AX", 0, 128), 0.0, A.mult, A.add)
+        if h == 1:
+            send(dst, (n, 0, 8), ("LO0", 0, 8), "num1")
+            arrive([(n, 0, 8)], "num1")
+            ts(("CMP", 128, 8 * PITCH, PITCH), ("I16", 0, 8), ("MF", 0, 1), A.add)
+            tt(("KMF", 0, 128), ("KI", 0, 128), ("MASK", 0, 128), A.mult)
+            ts(("KM", 0, 128), ("KMF", 0, 128), -4096.0, A.add)
+            for e in ("E1", "E2", "E3"):
+                fill((e, 0, 256), 1.0)
+            fill((r, 0, 128), float(rank))
+            fill((r, 128, 256), float(mate))
+            scopy((c, 0, 128), ("INV", 0, 128))
+            for o in range(O):
+                hold("y", [("XQ", 0, 256)], [])
+                load("y", ("WT", 512 * o, 512 * o + 512), T.w[:, 512 * o:512 * o + 512], "dw%d" % o)
+            for o in range(O):
+                quant(("WQ", 128 * o, 128 * o + 128), ("WS", 128 * o, 128 * o + 128), ("WT", 512 * o, 512 * o + 512))
+        else:
+            for i, b in enumerate((r, c)):
+                tt(("NX", 128 * i, 128 * i + 128), (b, 0, 128), ("MASK", 0, 128), A.mult)
+                scan(("NH", 128 * i, 128 * i + 128), ("HOLD", 0, 128), ("NX", 128 * i, 128 * i + 128), 0.0, A.mult, A.add)
+                copy(("NS%d" % h, 8 * i, 8 * i + 8), ("NH", 128 * i + 15, 128 * i + 128, 16))
+            send(dst, (n, 0, 16), ("NS%d" % h, 0, 16), "num%d" % h)
+            arrive([(n, 0, 16)], "num%d" % h)
+        if h == 3:
+            for o in range(O):
+                mm(("BY%d" % o, 0, 128), ("WQ", 128 * o, 128 * o + 128), ("WS", 128 * o, 128 * o + 128), *own)
+                scopy(("RES%d" % o, 0, 128), ("BY%d" % o, 0, 128))
+        mm(("BB", 0, 128), *U, *got)
+        if h == 3:
+            for o in range(O):
+                mm(("BS%d" % o, 0, 128), ("WQ", 128 * o, 128 * o + 128), ("WS", 128 * o, 128 * o + 128), *got)
+        beats = A.is_ge if rank & bit else A.is_gt
+        for b in range(8):
+            ts(("CMP", PITCH * b, PITCH * b + 128), ("BB", 0, 128), ("A16", 16 * b + 15, 16 * b + 16), beats)
+        for b in range(7):
+            accum(("CMP", PITCH * b, PITCH * b + 129), ("PA", b, b + 1))
+        last = ("CMP", PITCH * 7, PITCH * 7 + 129)
+        do("v", lambda: g.vector.tensor_reduce(ap(("PA", 7, 8)), ap(last), AxisListType.X, A.add), [("PA", 7, 8)], [last])
+        copy(("PAU", 0, 8), ("PA", 0, 8))
+        e, lo = "E%d" % h, ("LO%d" % h, 0, 8)
+        do("v", lambda: g.vector.tensor_copy(T[e][:, 0:256].indirect(T.PAU[:, 0:8]), T.ZB[:, 0:128]),
+           [(e, 0, 256)], [("PAU", 0, 8), ("ZB", 0, 128)])
+        scan(("TS", 0, 128), (e, 0, 128), ("ZB", 0, 128), 127.0, A.add, A.add)
+        ts(("EB", 0, 128), (e, 0, 128), 512.0, A.mult)
+        tt(("P1", 0, 128), ("EB", 0, 128), ("KM", 0, 128), A.add)
+        tt(("UU", 0, 128), ("P1", 0, 128), ("TS", 0, 128), A.subtract)
+        tt(("MX", 0, 128), ("UU", 0, 128), ("TS", 0, 128), A.min)
+        scan(("MH", 0, 128), ("HOLD", 0, 128), ("MX", 0, 128), 0.0, A.mult, A.max)
+        copy(lo, ("MH", 15, 128, 16))
+        if h == 3:
+            for o in range(O):
+                scopy(("RES%d" % o, 128, 256), ("BS%d" % o, 0, 128))
+        else:
+            pick_columns(("W%dQ" % (h + 1), 0, 128), ("W%dS" % (h + 1), 0, 128), (wq, 0, 256), (ws, 0, 256), lo)
+        if h == 1:
+            spick((c, 128, 256), ("J256", 0, 256), (n, 0, 8))
+        else:
+            spick((r, 128, 256), ("J256", 0, 256), (n, 0, 8))
+            spick((c, 128, 256), ("J256", 0, 256), (n, 8, 16))
+        if h < 3:
+            spick(("R%d" % (h + 1), 0, 128), (r, 0, 256), lo)
+            spick(("C%d" % (h + 1), 0, 128), (c, 0, 256), lo)
+        else:
+            vpick(("YB", 0, 128), ("RES0", 0, 256), lo)
+            spick(("YB", 128, 256), ("RES1", 0, 256), lo)
+            do("y", lambda: g.sync.dma_start(T.y[:, 0:128], ap(("YB", 0, 128))), [], [("YB", 0, 128)], "dy0", 16)
+            do("s", lambda: g.scalar.dma_start(T.y[:, 128:256], ap(("YB", 128, 256))), [], [("YB", 128, 256)], "dy1", 16)
+            vpick(("IDB", 0, 128), (r, 0, 256), lo)
+            vpick(("IDB", 128, 256), (c, 0, 256), lo)
+            do("y", lambda: g.sync.dma_start(T.id[:, :], T.IDB[0:1, 0:256]), [], [("IDB", 0, 256)], "did", 16)
+    for sem in sorted(total):
+        if known["g"].get(sem, 0) < total[sem]:
+            g.wait_ge(T.sem[sem], total[sem])

@@ -1,42 +1,39 @@
-from concourse.mybir import dt, AluOpType, AxisListType, ActivationFunctionType
+from concourse.bass import DstId, RemoteDMATransfer
+from concourse.mybir import dt, AluOpType, ActivationFunctionType
 
 N, T_COLS, K, O = 8, 256, 128, 2
 BF, F32, U16, I32, CODE, U8 = "bfloat16", "float32", "uint16", "int32", "float8_e4m3fn_x4", "uint8"
 PITCH = 144
 
-SCRATCH = {
-    "UT": ("sbuf", [128, 512], BF), "UQ0": ("sbuf", [128, 128], CODE), "US0": ("sbuf", [128, 128], U8),
-    "UQ": ("sbuf", [128, 128], CODE), "US": ("sbuf", [128, 128], U8), "UOFF": ("sbuf", [128, 8], U16),
-    "XT": ("sbuf", [128, 1024], BF), "XQ": ("sbuf", [128, 256], CODE), "XS": ("sbuf", [128, 256], U8),
-    "WT": ("sbuf", [128, 1024], BF), "WQ": ("sbuf", [128, 256], CODE), "WS": ("sbuf", [128, 256], U8),
-    "PIDX": ("sbuf", [128, 1], I32), "MI": ("sbuf", [128, 1], I32), "MF": ("sbuf", [128, 1], F32), "PF": ("sbuf", [128, 1], F32),
-    "TMOD": ("sbuf", [128, 256], BF), "MASK": ("sbuf", [128, 256], BF), "HOLD": ("sbuf", [128, 256], BF),
-    "J256": ("sbuf", [128, 256], BF), "JC": ("sbuf", [128, 256], BF), "KI": ("sbuf", [128, 128], F32),
-    "KMF": ("sbuf", [128, 128], F32), "KM": ("sbuf", [128, 128], BF), "I16": ("sbuf", [128, 8], F32),
-    "TRI": ("sbuf", [128, 128], BF), "ZB": ("sbuf", [128, 128], BF),
-    "CH0": ("sbuf", [128, 384], BF), "CH1": ("sbuf", [128, 384], BF), "EQ0": ("sbuf", [128, 128], BF), "EQ1": ("sbuf", [128, 128], BF),
-    "LR": ("sbuf", [128, 2], F32), "BX": ("sbuf", [128, 64], BF), "TR": ("sbuf", [128, 64], BF), "LRF": ("sbuf", [128, 256], BF),
-    "LX": ("sbuf", [128, 256], BF), "LH": ("sbuf", [128, 256], BF), "LU": ("sbuf", [128, 16], U16), "INV": ("sbuf", [128, 256], BF),
-    "IX": ("sbuf", [128, 128], BF), "IH": ("sbuf", [128, 128], BF), "LO0": ("sbuf", [128, 8], U16),
-    "AX": ("sbuf", [128, 128], F32), "A16": ("sbuf", [128, 128], F32), "CMP": ("sbuf", [128, 8 * PITCH], BF),
-    "PA": ("sbuf", [128, 8], F32), "PAU": ("sbuf", [128, 8], U16), "TS": ("sbuf", [128, 128], BF), "EB": ("sbuf", [128, 128], BF),
-    "P1": ("sbuf", [128, 128], BF), "UU": ("sbuf", [128, 128], BF), "MX": ("sbuf", [128, 128], BF), "MH": ("sbuf", [128, 128], BF),
-    "NX": ("sbuf", [128, 256], BF), "NH": ("sbuf", [128, 256], BF),
-    "RES0": ("sbuf", [128, 256], F32), "RES1": ("sbuf", [128, 256], F32), "YB": ("sbuf", [128, 256], F32), "IDB": ("sbuf", [128, 256], F32),
-    "BSF": ("psum", [128, 512], F32), "BS0": ("psum", [128, 512], F32), "BS1": ("psum", [128, 512], F32), "BA": ("psum", [128, 512], F32),
-    "BB": ("psum", [128, 512], F32), "BY0": ("psum", [128, 512], F32), "BY1": ("psum", [128, 512], F32),
-}
-for _h in (1, 2, 3):
-    SCRATCH["W%dQ" % _h] = ("sbuf", [128, 256], CODE)
-    SCRATCH["W%dS" % _h] = ("sbuf", [128, 256], U8)
-    SCRATCH["E%d" % _h] = ("sbuf", [128, 256], BF)
-    SCRATCH["LO%d" % _h] = ("sbuf", [128, 8], U16)
-    SCRATCH["R%d" % _h] = ("sbuf", [128, 256], BF)
-    SCRATCH["C%d" % _h] = ("sbuf", [128, 256], BF)
-    SCRATCH["NS%d" % _h] = ("sbuf", [128, 16], U16)
-    SCRATCH["NL%d" % _h] = ("sbuf", [128, 16], U16)
 
-PSUM_NAMES = [n for n in SCRATCH if SCRATCH[n][0] == "psum"]
+def _sbuf(cols, dtype, names):
+    return {n: ("sbuf", [128, cols], dtype) for n in names.split()}
+
+
+SCRATCH = {}
+SCRATCH.update(_sbuf(512, BF, "UT"))
+SCRATCH.update(_sbuf(1024, BF, "XT WT"))
+SCRATCH.update(_sbuf(128, CODE, "UQ0 UQ S2Q L2Q"))
+SCRATCH.update(_sbuf(128, U8, "US0 US S2S L2S"))
+SCRATCH.update(_sbuf(256, CODE, "XQ WQ W1Q W2Q W3Q"))
+SCRATCH.update(_sbuf(256, U8, "XS WS W1S W2S W3S"))
+SCRATCH.update(_sbuf(8, U16, "UOFF LO2 LO3 LOF PAU"))
+SCRATCH.update(_sbuf(16, U16, "LU NN ON PU OP NS3 NL3"))
+SCRATCH.update(_sbuf(8, I32, "PI PJ"))
+SCRATCH.update(_sbuf(1, I32, "PIDX MI"))
+SCRATCH.update(_sbuf(1, F32, "MF PF MF1 SC0 SC LR"))
+SCRATCH.update(_sbuf(8, F32, "I16 I16R PA"))
+SCRATCH.update(_sbuf(256, BF, "J256 JC TRI EQ LRF LH INV NX NH E1 E2 E3 R1 R2 R3 C1 C2 C3 RO CO"))
+SCRATCH.update(_sbuf(128, BF, "J128 TMOD MASK HOLD HE HB OWNV BASE ZB G GX FX FH TS UU MX MH"))
+SCRATCH.update(_sbuf(768, BF, "CH"))
+SCRATCH.update(_sbuf(192, BF, "LS"))
+SCRATCH.update(_sbuf(64, BF, "BX TR"))
+SCRATCH.update(_sbuf(8 * PITCH, BF, "CMP"))
+SCRATCH.update(_sbuf(130, BF, "PS"))
+SCRATCH.update(_sbuf(128, F32, "AFS AX A16"))
+SCRATCH.update(_sbuf(256, F32, "SW1 RES0 RES1 YB IDB"))
+PSUM_NAMES = ["BSF", "BS0", "BS1", "BA", "BB", "BY0", "BY1"]
+SCRATCH.update({n: ("psum", [128, 512], F32) for n in PSUM_NAMES})
 SEMAPHORES = ["v", "s", "t", "gc", "du", "dx0", "dx1", "dw0", "dw1", "dy0", "dy1", "did", "loc",
               "arr1", "arr2", "arr3", "num1", "num2", "num3"]
 
@@ -94,9 +91,13 @@ def rank_program(g, core, T, topo):
     def words(r):
         return ap(r).bitcast(dt.uint32)
 
-    def ts(out, in0, s, op):
+    def ts2(out, in0, s, s2, op0, op1):
         col = isinstance(s, tuple)
-        do("v", lambda: g.vector.tensor_scalar(ap(out), ap(in0), ap(s) if col else s, None, op), [out], [in0, s] if col else [in0])
+        last = () if op1 is None else (op1,)
+        do("v", lambda: g.vector.tensor_scalar(ap(out), ap(in0), ap(s) if col else s, s2, op0, *last), [out], [in0, s] if col else [in0])
+
+    def ts(out, in0, s, op):
+        ts2(out, in0, s, None, op, None)
 
     def tt(out, a, b, op):
         do("v", lambda: g.vector.tensor_tensor(ap(out), ap(a), ap(b), op), [out], [a, b])
@@ -113,12 +114,15 @@ def rank_program(g, core, T, topo):
     def vpick(out, win, off):
         do("v", lambda: g.vector.tensor_copy(ap(out), ap(win).indirect(ap(off))), [out], [win, off])
 
+    def vput(win, off, src):
+        do("v", lambda: g.vector.tensor_copy(ap(win).indirect(ap(off)), ap(src)), [win], [off, src])
+
     def spick(out, win, off):
         do("s", lambda: g.scalar.activation(ap(out), ap(win).indirect(ap(off)), F.Copy), [out], [win, off])
 
-    def pick_columns(q2, s2, q1, s1, off):
-        do("v", lambda: g.vector.tensor_copy(words(q2), words(q1).indirect(ap(off))), [q2], [q1, off])
-        spick(s2, s1, off)
+    def pick_columns(out, win, off):
+        do("v", lambda: g.vector.tensor_copy(words(out[0]), words(win[0]).indirect(ap(off))), [out[0]], [win[0], off])
+        spick(out[1], win[1], off)
 
     def fill(out, x):
         do("v", lambda: g.vector.memset(ap(out), x), [out], [])
@@ -135,20 +139,35 @@ def rank_program(g, core, T, topo):
     def accum(buf, out):
         do("s", lambda: g.scalar.activation(ap(buf), ap(buf), F.Identity, accum_out=ap(out)), [buf, out], [buf])
 
+    def off16(out, at, tmp, x, n):
+        scan((tmp, at, at + n), ("HB", 0, n), x, 0.0, A.mult, A.max)
+        ts2((out, at // 16, (at + n) // 16), (tmp, at + 15, at + n, 16), ("SC", 0, 1), 1.0, A.mult, A.subtract)
+
     def load(q, out, src, sem):
         do(q, lambda: engines[q].dma_start(ap(out), src), [out], [], sem, 16)
 
-    def send(dst, out, src, rsem, codes=False):
+    def sent(mate, rsem, copies=1):
+        n = len(topo.engines(core, T.cores[mate]))
+        total["loc"] = total.get("loc", 0) + n
+        total[rsem] = total.get(rsem, 0) + n * copies
+
+    def send(mate, out, src, rsem, codes=False):
+        dst = T.cores[mate]
         hold("g", [src], [])
         rid, pid = topo.addr(dst, core)
         a, b = (ap(out).bitcast(dt.uint8), ap(src).bitcast(dt.uint8)) if codes else (ap(out), ap(src))
         g.remote_dma(a, b, T.sem[rsem], T.sem["loc"], pid, rid, topo.mask(core, dst))
-        n = len(topo.engines(core, dst))
-        total["loc"] = total.get("loc", 0) + n
-        total[rsem] = total.get(rsem, 0) + n
+        sent(mate, rsem)
 
     def arrive(regions, sem):
         record([], regions, "-", sem, total[sem], {sem: total[sem]})
+
+    def exchange(mate, out, src, sem):
+        send(mate, out[0], src[0], sem, codes=True)
+        send(mate, out[1], src[1], sem)
+
+    def window(name, a, b):
+        return (name + "Q", a, b), (name + "S", a, b)
 
     load("y", ("UT", 0, 8), T.u[:, 0:8], "du")
     load("s", ("XT", 0, 512), T.x[:, 0:512], "dx0")
@@ -156,136 +175,193 @@ def rank_program(g, core, T, topo):
 
     fill(("UT", 8, 512), 0.0)
     fill(("UOFF", 0, 8), 0)
-    fill(("ZB", 0, 128), 0.0)
     iota(("PIDX", 0, 1), [[0, 1]], 0, 1)
-    iota(("TMOD", 0, 256), [[0, 16], [1, 16]], 0, 0)
-    iota(("J256", 0, 256), [[1, 256]], 0, 0)
-    iota(("JC", 0, 256), [[32, 4], [128, 2], [1, 32]], 0, 0)
-    iota(("I16", 0, 8), [[16, 8]], 0, 0)
-    iota(("KI", 0, 128), [[1, 128]], 127 + 4096, 0)
-    do("v", lambda: g.vector.tensor_scalar(ap(("MI", 0, 1)), ap(("PIDX", 0, 1)), 15, None, A.bitwise_and), [("MI", 0, 1)], [("PIDX", 0, 1)])
-    copy(("MF", 0, 1), ("MI", 0, 1))
+    iota(("J128", 0, 128), [[1, 128]], 0, 0)
+    iota(("TMOD", 0, 128), [[0, 8], [1, 16]], 0, 0)
+    iota(("JC", 0, 256), [[32, 4], [128, 2], [1, 32]], 1, 0)
+    ts(("MI", 0, 1), ("PIDX", 0, 1), 15, A.bitwise_and)
     copy(("PF", 0, 1), ("PIDX", 0, 1))
-    ts(("MASK", 0, 256), ("TMOD", 0, 256), ("MF", 0, 1), A.is_equal)
-    ts(("HOLD", 0, 256), ("TMOD", 0, 256), ("MF", 0, 1), A.is_gt)
-    ts(("TRI", 0, 128), ("J256", 0, 128), ("PF", 0, 1), A.is_lt)
+    copy(("MF", 0, 1), ("MI", 0, 1))
+    for h in (0, 1):
+        ts(("TRI", 128 * h, 128 * h + 128), ("J128", 0, 128), ("PF", 0, 1), A.is_lt)
 
     quant(("UQ0", 0, 128), ("US0", 0, 128), ("UT", 0, 512))
-    pick_columns(("UQ", 0, 128), ("US", 0, 128), ("UQ0", 0, 128), ("US0", 0, 128), ("UOFF", 0, 8))
     U = (("UQ", 0, 128), ("US", 0, 128))
+    pick_columns(U, (("UQ0", 0, 128), ("US0", 0, 128)), ("UOFF", 0, 8))
     for h in (0, 1):
         quant(("XQ", 128 * h, 128 * h + 128), ("XS", 128 * h, 128 * h + 128), ("XT", 512 * h, 512 * h + 512))
-    mm(("BS0", 0, 128), ("XQ", 0, 128), ("XS", 0, 128), *U)
-    mm(("BSF", 0, 256), *U, ("XQ", 0, 256), ("XS", 0, 256))
-    mm(("BS1", 0, 128), ("XQ", 128, 256), ("XS", 128, 256), *U)
+    mm(("BS0", 0, 128), *window("X", 0, 128), *U)
+    mm(("BSF", 0, 256), *U, *window("X", 0, 256))
+    mm(("BS1", 0, 128), *window("X", 128, 256), *U)
+    fill(("ZB", 0, 128), 0.0)
+    ts(("MF1", 0, 1), ("MF", 0, 1), 1.0, A.add)
+    ts2(("SC0", 0, 1), ("MF", 0, 1), 15.0, 255.0 / 256.0, A.is_equal, A.mult)
+    ts(("HOLD", 0, 128), ("TMOD", 0, 128), ("MF", 0, 1), A.is_gt)
+    ts2(("HE", 0, 128), ("TMOD", 0, 128), ("MF1", 0, 1), 255.0, A.is_equal, A.mult)
+    ts(("SC", 0, 1), ("SC0", 0, 1), 1.0 / 256.0, A.add)
+    tt(("HB", 0, 128), ("HOLD", 0, 128), ("HE", 0, 128), A.add)
 
+    high = rank & 1
     s0, s1 = ("BS0", 0, 1), ("BS1", 0, 1)
-    ts(("EQ0", 0, 128), ("BSF", 0, 128), s0, A.is_equal)
-    ts(("CH0", 0, 256), ("BSF", 0, 256), s0, A.is_gt)
-    tt(("CH0", 256, 384), ("EQ0", 0, 128), ("TRI", 0, 128), A.mult)
-    accum(("CH0", 0, 384), ("LR", 0, 1))
-    ts(("EQ1", 0, 128), ("BSF", 128, 256), s1, A.is_equal)
-    ts(("CH1", 0, 128), ("BSF", 0, 128), s1, A.is_ge)
-    ts(("CH1", 128, 256), ("BSF", 128, 256), s1, A.is_gt)
-    tt(("CH1", 256, 384), ("EQ1", 0, 128), ("TRI", 0, 128), A.mult)
-    accum(("CH1", 0, 384), ("LR", 1, 2))
-    for h in (0, 1):
-        ts(("BX", 32 * h, 32 * h + 32), ("ZB", 0, 32), ("LR", h, h + 1), A.add)
+    ts(("EQ", 0, 128), ("BSF", 0, 128), s0, A.is_equal)
+    ts(("EQ", 128, 256), ("BSF", 128, 256), s1, A.is_equal)
+    tt(("CH", 256, 512), ("EQ", 0, 256), ("TRI", 0, 256), A.mult)
+    ts(("CH", 0, 256), ("BSF", 0, 256), s0, A.is_gt)
+    accum(("CH", 0, 384), ("LR", 0, 1))
+    ts(("CH", 512, 640), ("BSF", 0, 128), s1, A.is_ge)
+    ts(("CH", 640, 768), ("BSF", 128, 256), s1, A.is_gt)
+    scan(("LS", 0, 192), ("CH", 384, 576), ("CH", 576, 768), 0.0, A.add, A.add)
+    for h, col in enumerate((("LR", 0, 1), ("LS", 191, 192))):
+        ts2(("BX", 32 * h, 32 * h + 32), ("ZB", 0, 32), col, 256.0 if high else 1.0, A.subtract if high else A.add, A.add)
     do("v", lambda: g.vector.transpose(ap(("TR", 0, 64)), ap(("BX", 0, 64))), [("TR", 0, 64)], [("BX", 0, 64)])
     for a in range(4):
         out = ("LRF", 64 * a, 64 * a + 64)
         do("g", lambda: g.partition_broadcast(ap(out), T.TR[32 * a:32 * a + 1, 0:64], 128), [out], [("TR", 0, 64)])
-    tt(("LX", 0, 256), ("LRF", 0, 256), ("MASK", 0, 256), A.mult)
-    scan(("LH", 0, 256), ("HOLD", 0, 256), ("LX", 0, 256), 0.0, A.mult, A.add)
-    copy(("LU", 0, 16), ("LH", 15, 256, 16))
-    do("v", lambda: g.vector.tensor_copy(T.INV[:, 0:256].indirect(T.LU[:, 0:16]), T.JC[:, 0:256]),
-       [("INV", 0, 256)], [("LU", 0, 16), ("JC", 0, 256)])
-    tt(("IX", 0, 128), ("INV", 0, 128), ("MASK", 0, 128), A.mult)
-    scan(("IH", 0, 128), ("HOLD", 0, 128), ("IX", 0, 128), 0.0, A.mult, A.add)
-    copy(("LO0", 0, 8), ("IH", 15, 128, 16))
-    pick_columns(("W1Q", 0, 128), ("W1S", 0, 128), ("XQ", 0, 256), ("XS", 0, 256), ("LO0", 0, 8))
+    for a in range(4):
+        off16("LU", 64 * a, "LH", ("LRF", 64 * a, 64 * a + 64), 64)
+        vput(("INV", 0, 256), ("LU", 4 * a, 4 * a + 4), ("JC", 64 * a, 64 * a + 64))
+    best = 128 if high else 0
+    a, z = (0, 128) if high else (128, 0)
+    off16("NN", a, "NH", ("INV", best, best + 128), 128)
+    mine, theirs = ("NN", a // 16, a // 16 + 8), ("NN", z // 16, z // 16 + 8)
+    own, got = window("W1", a, a + 128), window("W1", z, z + 128)
+    pick_columns(own, window("X", 0, 256), mine)
 
-    for h in (1, 2, 3):
-        wq, ws, n, c, r = "W%dQ" % h, "W%dS" % h, "NL%d" % h, "C%d" % h, "R%d" % h
-        own, got = ((wq, 0, 128), (ws, 0, 128)), ((wq, 128, 256), (ws, 128, 256))
-        bit = 1 << (h - 1)
-        mate = rank ^ bit
-        dst = T.cores[mate]
-        send(dst, got[0], own[0], "arr%d" % h, codes=True)
-        send(dst, got[1], own[1], "arr%d" % h)
-        arrive(got, "arr%d" % h)
-        mm(("BA", 0, 128), *U, *own)
-        tt(("AX", 0, 128), ("BA", 0, 128), ("MASK", 0, 128), A.mult)
+    def scores16(free):
+        tt(("AX", 0, 128), free, ("MASK", 0, 128), A.mult)
         scan(("A16", 0, 128), ("HOLD", 0, 128), ("AX", 0, 128), 0.0, A.mult, A.add)
-        if h == 1:
-            send(dst, (n, 0, 8), ("LO0", 0, 8), "num1")
-            arrive([(n, 0, 8)], "num1")
-            ts(("CMP", 128, 8 * PITCH, PITCH), ("I16", 0, 8), ("MF", 0, 1), A.add)
-            tt(("KMF", 0, 128), ("KI", 0, 128), ("MASK", 0, 128), A.mult)
-            ts(("KM", 0, 128), ("KMF", 0, 128), -4096.0, A.add)
-            for e in ("E1", "E2", "E3"):
-                fill((e, 0, 256), 1.0)
-            fill((r, 0, 128), float(rank))
-            fill((r, 128, 256), float(mate))
-            scopy((c, 0, 128), ("INV", 0, 128))
-            for o in range(O):
-                hold("y", [("XQ", 0, 256)], [])
-                load("y", ("WT", 512 * o, 512 * o + 512), T.w[:, 512 * o:512 * o + 512], "dw%d" % o)
-            for o in range(O):
-                quant(("WQ", 128 * o, 128 * o + 128), ("WS", 128 * o, 128 * o + 128), ("WT", 512 * o, 512 * o + 512))
-        else:
-            for i, b in enumerate((r, c)):
-                tt(("NX", 128 * i, 128 * i + 128), (b, 0, 128), ("MASK", 0, 128), A.mult)
-                scan(("NH", 128 * i, 128 * i + 128), ("HOLD", 0, 128), ("NX", 128 * i, 128 * i + 128), 0.0, A.mult, A.add)
-                copy(("NS%d" % h, 8 * i, 8 * i + 8), ("NH", 128 * i + 15, 128 * i + 128, 16))
-            send(dst, (n, 0, 16), ("NS%d" % h, 0, 16), "num%d" % h)
-            arrive([(n, 0, 16)], "num%d" % h)
+
+    def places(beats):
+        for b in range(8):
+            ts(("CMP", PITCH * b, PITCH * b + 128), ("BB", 0, 128), ("A16", 16 * b + 15, 16 * b + 16), beats)
+        for b in range(6):
+            accum(("CMP", PITCH * b, PITCH * b + 129), ("PA", b, b + 1))
+        for b in (6, 7):
+            y = PITCH * b
+            scan(("PS", 65 * (b - 6), 65 * (b - 6) + 65), ("CMP", y, y + 65), ("CMP", y + 65, y + 130), 0.0, A.add, A.add)
+        copy(("PAU", 6, 8), ("PS", 64, 130, 65))
+        copy(("PAU", 0, 6), ("PA", 0, 6))
+
+    mate = rank ^ 1
+    exchange(mate, own, own, "arr1")
+    arrive(got, "arr1")
+    hold("g", [mine], [])
+    four = [(rank ^ d, ap((name,) + mine[1:])) for d, name in ((1, "NN"), (2, "ON"), (3, "ON"))]
+    ids = [topo.addr(T.cores[m], core) for m, _ in four]
+    g.remote_dma_fused([RemoteDMATransfer(dst_ids=[DstId(rid=rid, pnc=pid) for rid, pid in ids], dma_engine_mask=topo.mask(core, T.cores[mate]),
+                                          remote_sem=T.sem["num1"], src=ap(mine), dsts=[d for _, d in four])], local_sem=T.sem["loc"])
+    sent(mate, "num1", 3)
+    arrive([theirs, ("ON", 0, 16)], "num1")
+    mm(("BA", 0, 128), *U, *own)
+    ts(("MASK", 0, 128), ("TMOD", 0, 128), ("MF", 0, 1), A.is_equal)
+    scopy(("SW1", a, a + 128), ("BA", 0, 128))
+    ts(("BASE", 0, 128), ("J128", 0, 128), a + 1.0, A.add)
+    scores16(("SW1", a, a + 128))
+    iota(("I16", 0, 8), [[16, 8]], 0, 0)
+    iota(("I16R", 0, 8), [[-16, 8]], 127, 0)
+    iota(("J256", 0, 256), [[1, 256]], 0, 0)
+    ts(("CMP", 128, 8 * PITCH, PITCH), ("I16R" if high else "I16", 0, 8), ("MF", 0, 1), A.subtract if high else A.add)
+    fill(("CMP", 129, 8 * PITCH, PITCH), 0.0)
+    ts(("OWNV", 0, 128), ("J128", 0, 128), 129.0, A.add)
+    for e in ("E1", "E2", "E3"):
+        fill((e, 0, 256), 4096.0 if e == "E1" and high else -4096.0)
+    for half in (0, 128):
+        up = 1 - half // 128
+        fill(("R1", half, half + 128), float((rank & ~1) + up))
+        fill(("RO", half, half + 128), float(((rank ^ 2) & ~1) + up))
+    ts(("C1", a, a + 128), ("INV", best, best + 128), 1.0, A.subtract)
+    for o in range(O):
+        hold("y", [("XQ", 0, 256)], [])
+        load("y", ("WT", 512 * o, 512 * o + 512), T.w[:, 512 * o:512 * o + 512], "dw%d" % o)
+    for o in range(O):
+        quant(("WQ", 128 * o, 128 * o + 128), ("WS", 128 * o, 128 * o + 128), ("WT", 512 * o, 512 * o + 512))
+    beats = A.is_ge if high else A.is_gt
+    mm(("BB", 0, 128), *U, *got)
+    tt(("G", 0, 128), ("BB", 0, 128), ("SW1", a, a + 128), beats)
+    ts(("GX", 0, 128), ("G", 0, 128), 128.0 if high else -128.0, A.mult)
+    tt(("FX", 0, 128), ("BASE", 0, 128), ("GX", 0, 128), A.add)
+    off16("LOF", 0, "FH", ("FX", 0, 128), 128)
+    pick_columns(window("S2", 0, 128), window("W1", 0, 256), ("LOF", 0, 8))
+    mate = rank ^ 2
+    exchange(mate, window("L2", 0, 128), window("S2", 0, 128), "arr2")
+    arrive(window("L2", 0, 128), "arr2")
+    places(beats)
+    scopy(("SW1", z, z + 128), ("BB", 0, 128))
+    vput(("E1", 0, 256), ("PAU", 0, 8), ("BASE", 0, 128))
+    pole = A.min if high else A.max
+    scan(("TS", 0, 128), ("E1", 0, 128), ("E1", 0, 128), 129.0 if high else 128.0, pole, pole)
+    tt(("UU", 0, 128), ("TS", 0, 128), ("J128", 0, 128), A.add if high else A.subtract)
+    tt(("MX", 0, 128), ("UU", 0, 128), ("E1", 0, 128), pole)
+    off16("PU", 128, "NX", ("MX", 0, 128), 128)
+    lo1 = ("PU", 8, 16)
+    spick(("AFS", 0, 128), ("SW1", 0, 256), lo1)
+    copy(("PI", 0, 8), lo1)
+    ts(("PJ", 0, 8), ("PI", 0, 8), 127, A.bitwise_and)
+    copy(("PU", 0, 8), ("PJ", 0, 8))
+    send(mate, ("OP", 0, 16), ("PU", 0, 16), "num2")
+    arrive([("OP", 0, 16)], "num2")
+    scores16(("AFS", 0, 128))
+    if high:
+        ts(("CMP", 128, 8 * PITCH, PITCH), ("I16", 0, 8), ("MF", 0, 1), A.add)
+    spick(("C1", z, z + 128), ("J256", 0, 256), theirs)
+    for half in (0, 128):
+        spick(("CO", half, half + 128), ("J256", 0, 256), ("ON", half // 16, half // 16 + 8))
+    spick(("R2", 128, 256), ("R1", 0, 256), lo1)
+    spick(("C2", 128, 256), ("C1", 0, 256), lo1)
+
+    for h in (2, 3):
+        w, c, r = "W%d" % h, "C%d" % h, "R%d" % h
+        own = window(w, 128, 256)
         if h == 3:
+            mate = rank ^ 4
+            got = window(w, 0, 128)
+            exchange(mate, got, own, "arr3")
+            arrive(got, "arr3")
+            mm(("BA", 0, 128), *U, *own)
+            scores16(("BA", 0, 128))
+            for i, b in enumerate((r, c)):
+                tt(("NX", 128 * i, 128 * i + 128), (b, 128, 256), ("MASK", 0, 128), A.mult)
+                scan(("NH", 128 * i, 128 * i + 128), ("HOLD", 0, 128), ("NX", 128 * i, 128 * i + 128), 0.0, A.mult, A.add)
+                copy(("NS3", 8 * i, 8 * i + 8), ("NH", 128 * i + 15, 128 * i + 128, 16))
+            send(mate, ("NL3", 0, 16), ("NS3", 0, 16), "num3")
+            arrive([("NL3", 0, 16)], "num3")
             for o in range(O):
-                mm(("BY%d" % o, 0, 128), ("WQ", 128 * o, 128 * o + 128), ("WS", 128 * o, 128 * o + 128), *own)
-                scopy(("RES%d" % o, 0, 128), ("BY%d" % o, 0, 128))
+                mm(("BY%d" % o, 0, 128), *window("W", 128 * o, 128 * o + 128), *own)
+                scopy(("RES%d" % o, 128, 256), ("BY%d" % o, 0, 128))
+        else:
+            got = window("L2", 0, 128)
         mm(("BB", 0, 128), *U, *got)
         if h == 3:
             for o in range(O):
-                mm(("BS%d" % o, 0, 128), ("WQ", 128 * o, 128 * o + 128), ("WS", 128 * o, 128 * o + 128), *got)
-        beats = A.is_ge if rank & bit else A.is_gt
-        for b in range(8):
-            ts(("CMP", PITCH * b, PITCH * b + 128), ("BB", 0, 128), ("A16", 16 * b + 15, 16 * b + 16), beats)
-        for b in range(7):
-            accum(("CMP", PITCH * b, PITCH * b + 129), ("PA", b, b + 1))
-        last = ("CMP", PITCH * 7, PITCH * 7 + 129)
-        do("v", lambda: g.vector.tensor_reduce(ap(("PA", 7, 8)), ap(last), AxisListType.X, A.add), [("PA", 7, 8)], [last])
-        copy(("PAU", 0, 8), ("PA", 0, 8))
-        e, lo = "E%d" % h, ("LO%d" % h, 0, 8)
-        do("v", lambda: g.vector.tensor_copy(T[e][:, 0:256].indirect(T.PAU[:, 0:8]), T.ZB[:, 0:128]),
-           [(e, 0, 256)], [("PAU", 0, 8), ("ZB", 0, 128)])
-        scan(("TS", 0, 128), (e, 0, 128), ("ZB", 0, 128), 127.0, A.add, A.add)
-        ts(("EB", 0, 128), (e, 0, 128), 512.0, A.mult)
-        tt(("P1", 0, 128), ("EB", 0, 128), ("KM", 0, 128), A.add)
-        tt(("UU", 0, 128), ("P1", 0, 128), ("TS", 0, 128), A.subtract)
-        tt(("MX", 0, 128), ("UU", 0, 128), ("TS", 0, 128), A.min)
-        scan(("MH", 0, 128), ("HOLD", 0, 128), ("MX", 0, 128), 0.0, A.mult, A.max)
-        copy(lo, ("MH", 15, 128, 16))
-        if h == 3:
+                mm(("BS%d" % o, 0, 128), *window("W", 128 * o, 128 * o + 128), *got)
+        places(A.is_ge if rank >> (h - 1) & 1 else A.is_gt)
+        e, lo = ("E%d" % h, 0, 128), ("LO%d" % h, 0, 8)
+        vput((e[0], 0, 256), ("PAU", 0, 8), ("OWNV", 0, 128))
+        if h == 2:
+            pick_columns(own, window("W1", 0, 256), lo1)
+        scan(("TS", 0, 128), e, e, 128.0, A.max, A.max)
+        tt(("UU", 0, 128), ("OWNV", 0, 128), ("TS", 0, 128), A.subtract)
+        tt(("MX", 0, 128), ("UU", 0, 128), e, A.max)
+        if h == 2:
+            pick_columns(window(w, 0, 128), got, ("OP", 0, 8))
+        off16("LO%d" % h, 0, "MH", ("MX", 0, 128), 128)
+        if h == 2:
+            pick_columns(window("W3", 128, 256), window(w, 0, 256), lo)
+            spick((r, 0, 128), ("RO", 0, 256), ("OP", 8, 16))
+            spick((c, 0, 128), ("CO", 0, 256), ("OP", 8, 16))
+            spick(("R3", 128, 256), (r, 0, 256), lo)
+            spick(("C3", 128, 256), (c, 0, 256), lo)
+        else:
             for o in range(O):
-                scopy(("RES%d" % o, 128, 256), ("BS%d" % o, 0, 128))
-        else:
-            pick_columns(("W%dQ" % (h + 1), 0, 128), ("W%dS" % (h + 1), 0, 128), (wq, 0, 256), (ws, 0, 256), lo)
-        if h == 1:
-            spick((c, 128, 256), ("J256", 0, 256), (n, 0, 8))
-        else:
-            spick((r, 128, 256), ("J256", 0, 256), (n, 0, 8))
-            spick((c, 128, 256), ("J256", 0, 256), (n, 8, 16))
-        if h < 3:
-            spick(("R%d" % (h + 1), 0, 128), (r, 0, 256), lo)
-            spick(("C%d" % (h + 1), 0, 128), (c, 0, 256), lo)
-        else:
+                scopy(("RES%d" % o, 0, 128), ("BS%d" % o, 0, 128))
             vpick(("YB", 0, 128), ("RES0", 0, 256), lo)
             spick(("YB", 128, 256), ("RES1", 0, 256), lo)
             do("y", lambda: g.sync.dma_start(T.y[:, 0:128], ap(("YB", 0, 128))), [], [("YB", 0, 128)], "dy0", 16)
-            do("s", lambda: g.scalar.dma_start(T.y[:, 128:256], ap(("YB", 128, 256))), [], [("YB", 128, 256)], "dy1", 16)
+            do("y", lambda: g.sync.dma_start(T.y[:, 128:256], ap(("YB", 128, 256))), [], [("YB", 128, 256)], "dy1", 16)
+            vpick((r, 0, 128), ("J256", 0, 256), ("NL3", 0, 8))
+            spick((c, 0, 128), ("J256", 0, 256), ("NL3", 8, 16))
             vpick(("IDB", 0, 128), (r, 0, 256), lo)
-            vpick(("IDB", 128, 256), (c, 0, 256), lo)
+            spick(("IDB", 128, 256), (c, 0, 256), lo)
             do("y", lambda: g.sync.dma_start(T.id[:, :], T.IDB[0:1, 0:256]), [], [("IDB", 0, 256)], "did", 16)
     for sem in sorted(total):
         if known["g"].get(sem, 0) < total[sem]:

@@ -29,12 +29,12 @@ SCRATCH.update(_sbuf(768, BF, "CH"))
 SCRATCH.update(_sbuf(192, BF, "LS"))
 SCRATCH.update(_sbuf(64, BF, "BX TR"))
 SCRATCH.update(_sbuf(8 * PITCH, BF, "CMP"))
-SCRATCH.update(_sbuf(130, BF, "PS"))
+SCRATCH.update(_sbuf(260, BF, "PS"))
 SCRATCH.update(_sbuf(128, F32, "AFS AX A16"))
 SCRATCH.update(_sbuf(256, F32, "SW1 RES0 RES1 YB IDB"))
 PSUM_NAMES = ["BSF", "BS0", "BS1", "BA", "BB", "BY0", "BY1"]
 SCRATCH.update({n: ("psum", [128, 512], F32) for n in PSUM_NAMES})
-SEMAPHORES = ["v", "s", "t", "gc", "du", "dx0", "dx1", "dw0", "dw1", "dy0", "dy1", "did", "loc",
+SEMAPHORES = ["v", "s", "t", "gc", "du", "dx0", "dx1", "dw0", "dw1", "dy", "did", "loc",
               "arr1", "arr2", "arr3", "num1", "num2", "num3"]
 
 
@@ -139,8 +139,10 @@ def rank_program(g, core, T, topo):
     def accum(buf, out):
         do("s", lambda: g.scalar.activation(ap(buf), ap(buf), F.Identity, accum_out=ap(out)), [buf, out], [buf])
 
-    def off16(out, at, tmp, x, n):
+    def off16(out, at, tmp, x, n, between=None):
         scan((tmp, at, at + n), ("HB", 0, n), x, 0.0, A.mult, A.max)
+        if between is not None:
+            between()
         ts2((out, at // 16, (at + n) // 16), (tmp, at + 15, at + n, 16), ("SC", 0, 1), 1.0, A.mult, A.subtract)
 
     def load(q, out, src, sem):
@@ -199,19 +201,19 @@ def rank_program(g, core, T, topo):
     ts(("HOLD", 0, 128), ("TMOD", 0, 128), ("MF", 0, 1), A.is_gt)
     ts2(("HE", 0, 128), ("TMOD", 0, 128), ("MF1", 0, 1), 255.0, A.is_equal, A.mult)
     ts(("SC", 0, 1), ("SC0", 0, 1), 1.0 / 256.0, A.add)
-    tt(("HB", 0, 128), ("HOLD", 0, 128), ("HE", 0, 128), A.add)
 
     high = rank & 1
     s0, s1 = ("BS0", 0, 1), ("BS1", 0, 1)
     ts(("EQ", 0, 128), ("BSF", 0, 128), s0, A.is_equal)
     ts(("EQ", 128, 256), ("BSF", 128, 256), s1, A.is_equal)
-    tt(("CH", 256, 512), ("EQ", 0, 256), ("TRI", 0, 256), A.mult)
     ts(("CH", 0, 256), ("BSF", 0, 256), s0, A.is_gt)
+    tt(("CH", 256, 512), ("EQ", 0, 256), ("TRI", 0, 256), A.mult)
     accum(("CH", 0, 384), ("LR", 0, 1))
     ts(("CH", 512, 640), ("BSF", 0, 128), s1, A.is_ge)
     ts(("CH", 640, 768), ("BSF", 128, 256), s1, A.is_gt)
+    tt(("HB", 0, 128), ("HOLD", 0, 128), ("HE", 0, 128), A.add)
     scan(("LS", 0, 192), ("CH", 384, 576), ("CH", 576, 768), 0.0, A.add, A.add)
-    for h, col in enumerate((("LR", 0, 1), ("LS", 191, 192))):
+    for h, col in ((0, ("LR", 0, 1)), (1, ("LS", 191, 192))):
         ts2(("BX", 32 * h, 32 * h + 32), ("ZB", 0, 32), col, 256.0 if high else 1.0, A.subtract if high else A.add, A.add)
     do("v", lambda: g.vector.transpose(ap(("TR", 0, 64)), ap(("BX", 0, 64))), [("TR", 0, 64)], [("BX", 0, 64)])
     for a in range(4):
@@ -220,6 +222,8 @@ def rank_program(g, core, T, topo):
     for a in range(4):
         off16("LU", 64 * a, "LH", ("LRF", 64 * a, 64 * a + 64), 64)
         vput(("INV", 0, 256), ("LU", 4 * a, 4 * a + 4), ("JC", 64 * a, 64 * a + 64))
+        if a == 0:
+            ts(("MASK", 0, 128), ("TMOD", 0, 128), ("MF", 0, 1), A.is_equal)
     best = 128 if high else 0
     a, z = (0, 128) if high else (128, 0)
     off16("NN", a, "NH", ("INV", best, best + 128), 128)
@@ -231,16 +235,20 @@ def rank_program(g, core, T, topo):
         tt(("AX", 0, 128), free, ("MASK", 0, 128), A.mult)
         scan(("A16", 0, 128), ("HOLD", 0, 128), ("AX", 0, 128), 0.0, A.mult, A.add)
 
-    def places(beats):
-        for b in range(8):
-            ts(("CMP", PITCH * b, PITCH * b + 128), ("BB", 0, 128), ("A16", 16 * b + 15, 16 * b + 16), beats)
-        for b in range(6):
+    def compare(b, beats):
+        ts(("CMP", PITCH * b, PITCH * b + 128), ("BB", 0, 128), ("A16", 16 * b + 15, 16 * b + 16), beats)
+
+    def places(beats, made=0, last=2):
+        for b in range(made, 8):
+            compare(b, beats)
+        k = 8 - last
+        for b in range(k):
             accum(("CMP", PITCH * b, PITCH * b + 129), ("PA", b, b + 1))
-        for b in (6, 7):
-            y = PITCH * b
-            scan(("PS", 65 * (b - 6), 65 * (b - 6) + 65), ("CMP", y, y + 65), ("CMP", y + 65, y + 130), 0.0, A.add, A.add)
-        copy(("PAU", 6, 8), ("PS", 64, 130, 65))
-        copy(("PAU", 0, 6), ("PA", 0, 6))
+        for b in range(k, 8):
+            y, p = PITCH * b, 65 * (b - k)
+            scan(("PS", p, p + 65), ("CMP", y, y + 65), ("CMP", y + 65, y + 130), 0.0, A.add, A.add)
+        copy(("PAU", k, 8), ("PS", 64, 65 * last, 65))
+        copy(("PAU", 0, k), ("PA", 0, k))
 
     mate = rank ^ 1
     exchange(mate, own, own, "arr1")
@@ -253,39 +261,40 @@ def rank_program(g, core, T, topo):
     sent(mate, "num1", 3)
     arrive([theirs, ("ON", 0, 16)], "num1")
     mm(("BA", 0, 128), *U, *own)
-    ts(("MASK", 0, 128), ("TMOD", 0, 128), ("MF", 0, 1), A.is_equal)
     scopy(("SW1", a, a + 128), ("BA", 0, 128))
     ts(("BASE", 0, 128), ("J128", 0, 128), a + 1.0, A.add)
+    fill(("E1", 0, 256), 4096.0 if high else -4096.0)
+    fill(("CMP", 129, 8 * PITCH, PITCH), 0.0)
     scores16(("SW1", a, a + 128))
     iota(("I16", 0, 8), [[16, 8]], 0, 0)
     iota(("I16R", 0, 8), [[-16, 8]], 127, 0)
     iota(("J256", 0, 256), [[1, 256]], 0, 0)
     ts(("CMP", 128, 8 * PITCH, PITCH), ("I16R" if high else "I16", 0, 8), ("MF", 0, 1), A.subtract if high else A.add)
-    fill(("CMP", 129, 8 * PITCH, PITCH), 0.0)
+    for o in range(O):
+        hold("y", [("XQ", 0, 256)], [])
+        load("y", ("WT", 512 * o, 512 * o + 512), T.w[:, 512 * o:512 * o + 512], "dw%d" % o)
+    fill(("E2", 0, 256), -4096.0)
     ts(("OWNV", 0, 128), ("J128", 0, 128), 129.0, A.add)
-    for e in ("E1", "E2", "E3"):
-        fill((e, 0, 256), 4096.0 if e == "E1" and high else -4096.0)
     for half in (0, 128):
         up = 1 - half // 128
         fill(("R1", half, half + 128), float((rank & ~1) + up))
         fill(("RO", half, half + 128), float(((rank ^ 2) & ~1) + up))
     ts(("C1", a, a + 128), ("INV", best, best + 128), 1.0, A.subtract)
-    for o in range(O):
-        hold("y", [("XQ", 0, 256)], [])
-        load("y", ("WT", 512 * o, 512 * o + 512), T.w[:, 512 * o:512 * o + 512], "dw%d" % o)
-    for o in range(O):
-        quant(("WQ", 128 * o, 128 * o + 128), ("WS", 128 * o, 128 * o + 128), ("WT", 512 * o, 512 * o + 512))
     beats = A.is_ge if high else A.is_gt
     mm(("BB", 0, 128), *U, *got)
     tt(("G", 0, 128), ("BB", 0, 128), ("SW1", a, a + 128), beats)
+    compare(0, beats)
     ts(("GX", 0, 128), ("G", 0, 128), 128.0 if high else -128.0, A.mult)
+    compare(1, beats)
     tt(("FX", 0, 128), ("BASE", 0, 128), ("GX", 0, 128), A.add)
-    off16("LOF", 0, "FH", ("FX", 0, 128), 128)
+    compare(2, beats)
+    off16("LOF", 0, "FH", ("FX", 0, 128), 128, lambda: compare(3, beats))
+    compare(4, beats)
     pick_columns(window("S2", 0, 128), window("W1", 0, 256), ("LOF", 0, 8))
     mate = rank ^ 2
     exchange(mate, window("L2", 0, 128), window("S2", 0, 128), "arr2")
     arrive(window("L2", 0, 128), "arr2")
-    places(beats)
+    places(beats, 5, 4)
     scopy(("SW1", z, z + 128), ("BB", 0, 128))
     vput(("E1", 0, 256), ("PAU", 0, 8), ("BASE", 0, 128))
     pole = A.min if high else A.max
@@ -295,14 +304,14 @@ def rank_program(g, core, T, topo):
     off16("PU", 128, "NX", ("MX", 0, 128), 128)
     lo1 = ("PU", 8, 16)
     spick(("AFS", 0, 128), ("SW1", 0, 256), lo1)
-    copy(("PI", 0, 8), lo1)
+    ts2(("PI", 0, 8), ("NX", 143, 256, 16), ("SC", 0, 1), 1.0, A.mult, A.subtract)
+    if high:
+        ts(("CMP", 128, 8 * PITCH, PITCH), ("I16", 0, 8), ("MF", 0, 1), A.add)
     ts(("PJ", 0, 8), ("PI", 0, 8), 127, A.bitwise_and)
     copy(("PU", 0, 8), ("PJ", 0, 8))
     send(mate, ("OP", 0, 16), ("PU", 0, 16), "num2")
     arrive([("OP", 0, 16)], "num2")
     scores16(("AFS", 0, 128))
-    if high:
-        ts(("CMP", 128, 8 * PITCH, PITCH), ("I16", 0, 8), ("MF", 0, 1), A.add)
     spick(("C1", z, z + 128), ("J256", 0, 256), theirs)
     for half in (0, 128):
         spick(("CO", half, half + 128), ("J256", 0, 256), ("ON", half // 16, half // 16 + 8))
@@ -318,11 +327,17 @@ def rank_program(g, core, T, topo):
             exchange(mate, got, own, "arr3")
             arrive(got, "arr3")
             mm(("BA", 0, 128), *U, *own)
+            fill(("E3", 0, 256), -4096.0)
+            for o in range(O):
+                quant(("WQ", 128 * o, 128 * o + 128), ("WS", 128 * o, 128 * o + 128), ("WT", 512 * o, 512 * o + 512))
             scores16(("BA", 0, 128))
-            for i, b in enumerate((r, c)):
-                tt(("NX", 128 * i, 128 * i + 128), (b, 128, 256), ("MASK", 0, 128), A.mult)
-                scan(("NH", 128 * i, 128 * i + 128), ("HOLD", 0, 128), ("NX", 128 * i, 128 * i + 128), 0.0, A.mult, A.add)
-                copy(("NS3", 8 * i, 8 * i + 8), ("NH", 128 * i + 15, 128 * i + 128, 16))
+            lists = [((128 * i, 128 * i + 128), b) for i, b in enumerate((r, c))]
+            for at, b in lists:
+                tt(("NX",) + at, (b, 128, 256), ("MASK", 0, 128), A.mult)
+            for at, b in lists:
+                scan(("NH",) + at, ("HOLD", 0, 128), ("NX",) + at, 0.0, A.mult, A.add)
+            for at, b in lists:
+                copy(("NS3", at[0] // 16, at[1] // 16), ("NH", at[0] + 15, at[1], 16))
             send(mate, ("NL3", 0, 16), ("NS3", 0, 16), "num3")
             arrive([("NL3", 0, 16)], "num3")
             for o in range(O):
@@ -354,15 +369,15 @@ def rank_program(g, core, T, topo):
         else:
             for o in range(O):
                 scopy(("RES%d" % o, 0, 128), ("BS%d" % o, 0, 128))
+            spick((r, 0, 128), ("J256", 0, 256), ("NL3", 0, 8))
+            spick((c, 0, 128), ("J256", 0, 256), ("NL3", 8, 16))
             vpick(("YB", 0, 128), ("RES0", 0, 256), lo)
             spick(("YB", 128, 256), ("RES1", 0, 256), lo)
-            do("y", lambda: g.sync.dma_start(T.y[:, 0:128], ap(("YB", 0, 128))), [], [("YB", 0, 128)], "dy0", 16)
-            do("y", lambda: g.sync.dma_start(T.y[:, 128:256], ap(("YB", 128, 256))), [], [("YB", 128, 256)], "dy1", 16)
-            vpick((r, 0, 128), ("J256", 0, 256), ("NL3", 0, 8))
-            spick((c, 0, 128), ("J256", 0, 256), ("NL3", 8, 16))
+            do("y", lambda: g.sync.dma_start(T.y[:, :], ap(("YB", 0, 256))), [], [("YB", 0, 256)], "dy", 16)
             vpick(("IDB", 0, 128), (r, 0, 256), lo)
             spick(("IDB", 128, 256), (c, 0, 256), lo)
-            do("y", lambda: g.sync.dma_start(T.id[:, :], T.IDB[0:1, 0:256]), [], [("IDB", 0, 256)], "did", 16)
-    for sem in sorted(total):
+            do("s", lambda: g.scalar.dma_start(T.id[:, :], T.IDB[0:1, 0:256]), [], [("IDB", 0, 256)], "did", 16)
+    late = ("t", "v", "s", "did", "dy")
+    for sem in sorted(x for x in total if x not in late) + list(late):
         if known["g"].get(sem, 0) < total[sem]:
             g.wait_ge(T.sem[sem], total[sem])

@@ -3,7 +3,8 @@ from concourse.mybir import dt, AluOpType, ActivationFunctionType
 
 N, T_COLS, K, O = 8, 256, 128, 2
 BF, F32, U16, I32, CODE, U8 = "bfloat16", "float32", "uint16", "int32", "float8_e4m3fn_x4", "uint8"
-PITCH = 144
+OTH = 64 * (N - 1)
+ZC = 16
 
 
 def _sbuf(cols, dtype, names):
@@ -12,30 +13,42 @@ def _sbuf(cols, dtype, names):
 
 SCRATCH = {}
 SCRATCH.update(_sbuf(512, BF, "UT"))
-SCRATCH.update(_sbuf(1024, BF, "XT WT"))
-SCRATCH.update(_sbuf(128, CODE, "UQ0 UQ S2Q L2Q"))
-SCRATCH.update(_sbuf(128, U8, "US0 US S2S L2S"))
-SCRATCH.update(_sbuf(256, CODE, "XQ WQ W1Q W2Q W3Q"))
-SCRATCH.update(_sbuf(256, U8, "XS WS W1S W2S W3S"))
-SCRATCH.update(_sbuf(8, U16, "UOFF LO2 LO3 LOF PAU"))
-SCRATCH.update(_sbuf(16, U16, "LU NN ON PU OP NS3 NL3"))
-SCRATCH.update(_sbuf(8, I32, "PI PJ"))
-SCRATCH.update(_sbuf(1, I32, "PIDX MI"))
-SCRATCH.update(_sbuf(1, F32, "MF PF MF1 SC0 SC LR"))
-SCRATCH.update(_sbuf(8, F32, "I16 I16R PA"))
-SCRATCH.update(_sbuf(256, BF, "J256 JC TRI EQ LRF LH INV NX NH E1 E2 E3 R1 R2 R3 C1 C2 C3 RO CO"))
-SCRATCH.update(_sbuf(128, BF, "J128 TMOD MASK HOLD HE HB OWNV BASE ZB G GX FX FH TS UU MX MH"))
+SCRATCH.update(_sbuf(1024 + 4 * ZC, BF, "XT"))
+SCRATCH.update(_sbuf(1024, BF, "WT"))
+SCRATCH.update(_sbuf(128, CODE, "UQ0 UQ V4Q L4Q"))
+SCRATCH.update(_sbuf(128, U8, "US0 US V4S L4S"))
+SCRATCH.update(_sbuf(256, CODE, "WQ W1Q"))
+SCRATCH.update(_sbuf(256, U8, "WS W1S"))
+SCRATCH.update(_sbuf(256 + ZC, CODE, "XQ ZQ"))
+SCRATCH.update(_sbuf(256 + ZC, U8, "XS ZS"))
+SCRATCH.update(_sbuf(8, U16, "UOFF NN LOF LUG LC LID LIA"))
+SCRATCH.update(_sbuf(2, U16, "ZOFF"))
+SCRATCH.update(_sbuf(16, U16, "LU"))
+SCRATCH.update(_sbuf(32, U16, "LV4"))
+SCRATCH.update(_sbuf(4 * (N - 1), U16, "GOFF"))
+SCRATCH.update(_sbuf(4 * (N - 1), BF, "GO"))
+SCRATCH.update(_sbuf(1, I32, "PIDX MI MJ"))
+SCRATCH.update(_sbuf(8, I32, "FO TM TC TK NI"))
+SCRATCH.update(_sbuf(16, I32, "MO SM"))
+SCRATCH.update(_sbuf(32, I32, "VI AN GN SN"))
+SCRATCH.update(_sbuf(1, F32, "MF PF MF1 SC0 SC LR PM"))
+SCRATCH.update(_sbuf(2, F32, "SCO"))
+SCRATCH.update(_sbuf(16, F32, "SCR"))
+SCRATCH.update(_sbuf(4, F32, "PG X1 P2 X2 P3 K128"))
+SCRATCH.update(_sbuf(256, BF, "JC TRI EQ LRF LH INV IDO IDA"))
+SCRATCH.update(_sbuf(128, BF, "J128 TMOD HOLD HE HB BASE ZB G GX FX FH NH CB KCB BXG GFX GH"))
+SCRATCH.update(_sbuf(1280, BF, "RTO RTA CT"))
 SCRATCH.update(_sbuf(768, BF, "CH"))
 SCRATCH.update(_sbuf(192, BF, "LS"))
-SCRATCH.update(_sbuf(64, BF, "BX TR"))
-SCRATCH.update(_sbuf(8 * PITCH, BF, "CMP"))
-SCRATCH.update(_sbuf(260, BF, "PS"))
-SCRATCH.update(_sbuf(128, F32, "AFS AX A16"))
-SCRATCH.update(_sbuf(256, F32, "SW1 RES0 RES1 YB IDB"))
+SCRATCH.update(_sbuf(64, BF, "BX"))
+SCRATCH.update(_sbuf(4 * OTH, BF, "CM"))
+SCRATCH.update(_sbuf(OTH, F32, "EX0 EX"))
+SCRATCH.update(_sbuf(128, F32, "ST SW VC VAL EH"))
+SCRATCH.update(_sbuf(256, F32, "E1 YB IDB"))
 PSUM_NAMES = ["BSF", "BS0", "BS1", "BA", "BB", "BY0", "BY1"]
 SCRATCH.update({n: ("psum", [128, 512], F32) for n in PSUM_NAMES})
 SEMAPHORES = ["v", "s", "t", "gc", "du", "dx0", "dx1", "dw0", "dw1", "dy", "did", "loc",
-              "arr1", "arr2", "arr3", "num1", "num2", "num3"]
+              "arr1", "arr2", "arr3", "sc", "num1", "num3"]
 
 
 def rank_program(g, core, T, topo):
@@ -49,18 +62,22 @@ def rank_program(g, core, T, topo):
     total = {}
     hist = {}
 
+    def parts(r):
+        return (r[4], r[5]) if len(r) > 4 else (0, 128)
+
     def record(reads, writes, q, sem, val, clock):
         for rs, w in ((reads, False), (writes, True)):
             for r in rs:
-                hist.setdefault(r[0], []).append((r[1], r[2], w, q, sem, val, clock))
+                hist.setdefault(r[0], []).append((r[1], r[2]) + parts(r) + (w, q, sem, val, clock))
 
     def hold(q, reads, writes):
         need = {}
         for rs, w in ((reads, False), (writes, True)):
             for r in rs:
                 psum = r[0] in PSUM_NAMES
-                for lo, hi, hw, hq, sem, val, clock in hist.get(r[0], []):
-                    if not (psum or (lo < r[2] and r[1] < hi)):
+                a, z = parts(r)
+                for lo, hi, p0, p1, hw, hq, sem, val, clock in hist.get(r[0], []):
+                    if not (psum or (lo < r[2] and r[1] < hi and p0 < z and a < p1)):
                         continue
                     if not (w or hw or (psum and hq != q)):
                         continue
@@ -86,15 +103,19 @@ def rank_program(g, core, T, topo):
         record(reads, writes, q, sem, total[sem], clock)
 
     def ap(r):
-        return T[r[0]][:, r[1]:r[2]] if len(r) == 3 else T[r[0]][:, r[1]:r[2]:r[3]]
+        if len(r) == 3:
+            return T[r[0]][:, r[1]:r[2]]
+        p, z = parts(r)
+        return T[r[0]][p:z, r[1]:r[2]:r[3]]
 
     def words(r):
         return ap(r).bitcast(dt.uint32)
 
     def ts2(out, in0, s, s2, op0, op1):
-        col = isinstance(s, tuple)
+        cols = [x for x in (s, s2) if isinstance(x, tuple)]
+        a, b = [ap(x) if isinstance(x, tuple) else x for x in (s, s2)]
         last = () if op1 is None else (op1,)
-        do("v", lambda: g.vector.tensor_scalar(ap(out), ap(in0), ap(s) if col else s, s2, op0, *last), [out], [in0, s] if col else [in0])
+        do("v", lambda: g.vector.tensor_scalar(ap(out), ap(in0), a, b, op0, *last), [out], [in0] + cols)
 
     def ts(out, in0, s, op):
         ts2(out, in0, s, None, op, None)
@@ -104,6 +125,9 @@ def rank_program(g, core, T, topo):
 
     def scan(out, a, b, init, op0, op1):
         do("v", lambda: g.vector.tensor_tensor_scan(ap(out), ap(a), ap(b), init, op0, op1), [out], [a, b])
+
+    def turn(out, a):
+        do("v", lambda: g.vector.transpose(ap(out), ap(a)), [out], [a])
 
     def copy(out, a):
         do("v", lambda: g.vector.tensor_copy(ap(out), ap(a)), [out], [a])
@@ -133,17 +157,17 @@ def rank_program(g, core, T, topo):
     def quant(q, s, t):
         do("v", lambda: g.vector.quantize_mx(ap(q), ap(s), ap(t)), [q, s], [t])
 
-    def mm(out, wq, ws, xq, xs):
-        do("t", lambda: g.tensor.matmul_mx(ap(out), ap(wq), ap(ws), ap(xq), ap(xs), True, True), [out], [wq, ws, xq, xs])
+    def mm(out, wq, ws, xq, xs, start=True, stop=True):
+        do("t", lambda: g.tensor.matmul_mx(ap(out), ap(wq), ap(ws), ap(xq), ap(xs), start, stop), [out], [wq, ws, xq, xs])
 
     def accum(buf, out):
         do("s", lambda: g.scalar.activation(ap(buf), ap(buf), F.Identity, accum_out=ap(out)), [buf, out], [buf])
 
-    def off16(out, at, tmp, x, n, between=None):
-        scan((tmp, at, at + n), ("HB", 0, n), x, 0.0, A.mult, A.max)
-        if between is not None:
-            between()
-        ts2((out, at // 16, (at + n) // 16), (tmp, at + 15, at + n, 16), ("SC", 0, 1), 1.0, A.mult, A.subtract)
+    def hold16(tmp, x):
+        scan(tmp, ("HB", 0, tmp[2] - tmp[1]), x, 0.0, A.mult, A.max)
+
+    def take16(out, tmp, less):
+        ts2(out, (tmp[0], tmp[1] + 15, tmp[2], 16), ("SC", 0, 1), less, A.mult, A.subtract)
 
     def load(q, out, src, sem):
         do(q, lambda: engines[q].dma_start(ap(out), src), [out], [], sem, 16)
@@ -161,6 +185,14 @@ def rank_program(g, core, T, topo):
         g.remote_dma(a, b, T.sem[rsem], T.sem["loc"], pid, rid, topo.mask(core, dst))
         sent(mate, rsem)
 
+    def spread(mates, outs, src, rsem):
+        hold("g", [src], [])
+        ids = [topo.addr(T.cores[m], core) for m in mates]
+        g.remote_dma_fused([RemoteDMATransfer(
+            dst_ids=[DstId(rid=rid, pnc=pid) for rid, pid in ids], dma_engine_mask=topo.mask(core, T.cores[mates[0]]),
+            remote_sem=T.sem[rsem], src=ap(src), dsts=[ap(o) for o in outs])], local_sem=T.sem["loc"])
+        sent(mates[0], rsem, len(mates))
+
     def arrive(regions, sem):
         record([], regions, "-", sem, total[sem], {sem: total[sem]})
 
@@ -171,30 +203,46 @@ def rank_program(g, core, T, topo):
     def window(name, a, b):
         return (name + "Q", a, b), (name + "S", a, b)
 
+    high = rank & 1
+
     load("y", ("UT", 0, 8), T.u[:, 0:8], "du")
     load("s", ("XT", 0, 512), T.x[:, 0:512], "dx0")
     load("y", ("XT", 512, 1024), T.x[:, 512:1024], "dx1")
 
     fill(("UT", 8, 512), 0.0)
+    fill(("XT", 1024, 1024 + 4 * ZC), 0.0)
     fill(("UOFF", 0, 8), 0)
     iota(("PIDX", 0, 1), [[0, 1]], 0, 1)
     iota(("J128", 0, 128), [[1, 128]], 0, 0)
     iota(("TMOD", 0, 128), [[0, 8], [1, 16]], 0, 0)
     iota(("JC", 0, 256), [[32, 4], [128, 2], [1, 32]], 1, 0)
+    if rank:
+        iota(("GO", 0, 4 * rank), [[1, 2 * rank], [0, 2]], 0, 0)
+    if rank < N - 1:
+        iota(("GO", 4 * rank, 4 * (N - 1)), [[1, 2 * (N - 1 - rank)], [0, 2]], 2 * rank + 2, 0)
     ts(("MI", 0, 1), ("PIDX", 0, 1), 15, A.bitwise_and)
+    ts(("MJ", 0, 1), ("PIDX", 0, 1), 31, A.bitwise_and)
     copy(("PF", 0, 1), ("PIDX", 0, 1))
     copy(("MF", 0, 1), ("MI", 0, 1))
+    copy(("PM", 0, 1), ("MJ", 0, 1))
     for h in (0, 1):
         ts(("TRI", 128 * h, 128 * h + 128), ("J128", 0, 128), ("PF", 0, 1), A.is_lt)
 
     quant(("UQ0", 0, 128), ("US0", 0, 128), ("UT", 0, 512))
     U = (("UQ", 0, 128), ("US", 0, 128))
     pick_columns(U, (("UQ0", 0, 128), ("US0", 0, 128)), ("UOFF", 0, 8))
+    quant(("XQ", 0, 128), ("XS", 0, 128), ("XT", 0, 512))
+    quant(("XQ", 128, 256 + ZC), ("XS", 128, 256 + ZC), ("XT", 512, 1024 + 4 * ZC))
     for h in (0, 1):
-        quant(("XQ", 128 * h, 128 * h + 128), ("XS", 128 * h, 128 * h + 128), ("XT", 512 * h, 512 * h + 512))
-    mm(("BS0", 0, 128), *window("X", 0, 128), *U)
-    mm(("BSF", 0, 256), *U, *window("X", 0, 256))
+        mm(("BY%d" % h, 0, 128), *window("X", 128 * h, 128 * h + 128), *U)
+        scopy(("SCO", h, h + 1), ("BY%d" % h, 0, 1))
+        if h == 0:
+            mm(("BS0", 0, 128), *window("X", 0, 128), *U)
+            mm(("BSF", 0, 256), *U, *window("X", 0, 256))
     mm(("BS1", 0, 128), *window("X", 128, 256), *U)
+    others = [s for s in range(N) if s != rank]
+    spread(others, [("SCR", 2 * rank, 2 * rank + 2)] * (N - 1), ("SCO", 0, 2), "sc")
+    arrive([("SCR", 0, 16)], "sc")
     fill(("ZB", 0, 128), 0.0)
     ts(("MF1", 0, 1), ("MF", 0, 1), 1.0, A.add)
     ts2(("SC0", 0, 1), ("MF", 0, 1), 15.0, 255.0 / 256.0, A.is_equal, A.mult)
@@ -202,7 +250,6 @@ def rank_program(g, core, T, topo):
     ts2(("HE", 0, 128), ("TMOD", 0, 128), ("MF1", 0, 1), 255.0, A.is_equal, A.mult)
     ts(("SC", 0, 1), ("SC0", 0, 1), 1.0 / 256.0, A.add)
 
-    high = rank & 1
     s0, s1 = ("BS0", 0, 1), ("BS1", 0, 1)
     ts(("EQ", 0, 128), ("BSF", 0, 128), s0, A.is_equal)
     ts(("EQ", 128, 256), ("BSF", 128, 256), s1, A.is_equal)
@@ -213,170 +260,136 @@ def rank_program(g, core, T, topo):
     ts(("CH", 640, 768), ("BSF", 128, 256), s1, A.is_gt)
     tt(("HB", 0, 128), ("HOLD", 0, 128), ("HE", 0, 128), A.add)
     scan(("LS", 0, 192), ("CH", 384, 576), ("CH", 576, 768), 0.0, A.add, A.add)
+    copy(("GOFF", 0, 4 * (N - 1)), ("GO", 0, 4 * (N - 1)))
     for h, col in ((0, ("LR", 0, 1)), (1, ("LS", 191, 192))):
         ts2(("BX", 32 * h, 32 * h + 32), ("ZB", 0, 32), col, 256.0 if high else 1.0, A.subtract if high else A.add, A.add)
-    do("v", lambda: g.vector.transpose(ap(("TR", 0, 64)), ap(("BX", 0, 64))), [("TR", 0, 64)], [("BX", 0, 64)])
+
+    def quad(name, a, b, p, n=32):
+        return (name, a, b, 1, p, p + n)
+
     for a in range(4):
-        out = ("LRF", 64 * a, 64 * a + 64)
-        do("g", lambda: g.partition_broadcast(ap(out), T.TR[32 * a:32 * a + 1, 0:64], 128), [out], [("TR", 0, 64)])
+        turn(quad("LRF", 64 * a, 64 * a + 64, 32 * a), quad("BX", 0, 64, 32 * a))
     for a in range(4):
-        off16("LU", 64 * a, "LH", ("LRF", 64 * a, 64 * a + 64), 64)
-        vput(("INV", 0, 256), ("LU", 4 * a, 4 * a + 4), ("JC", 64 * a, 64 * a + 64))
-        if a == 0:
-            ts(("MASK", 0, 128), ("TMOD", 0, 128), ("MF", 0, 1), A.is_equal)
+        c = (64 * a, 64 * a + 64)
+        (copy if a < 2 else scopy)(quad("LRF", *c, 32 * (a ^ 1)), quad("LRF", *c, 32 * a))
+    copy(quad("LRF", 0, 128, 64, 64), quad("LRF", 0, 128, 0, 64))
+    scopy(quad("LRF", 128, 256, 0, 64), quad("LRF", 128, 256, 64, 64))
+    for a in (0, 128):
+        hold16(("LH", a, a + 128), ("LRF", a, a + 128))
+    for a in (0, 128):
+        take16(("LU", a // 16, a // 16 + 8), ("LH", a, a + 128), 1.0)
+    vput(("INV", 0, 256), ("LU", 0, 16), ("JC", 0, 256))
     best = 128 if high else 0
     a, z = (0, 128) if high else (128, 0)
-    off16("NN", a, "NH", ("INV", best, best + 128), 128)
-    mine, theirs = ("NN", a // 16, a // 16 + 8), ("NN", z // 16, z // 16 + 8)
+    hold16(("NH", 0, 128), ("INV", best, best + 128))
+    take16(("NN", 0, 8), ("NH", 0, 128), 1.0)
     own, got = window("W1", a, a + 128), window("W1", z, z + 128)
-    pick_columns(own, window("X", 0, 256), mine)
-
-    def scores16(free):
-        tt(("AX", 0, 128), free, ("MASK", 0, 128), A.mult)
-        scan(("A16", 0, 128), ("HOLD", 0, 128), ("AX", 0, 128), 0.0, A.mult, A.add)
-
-    def compare(b, beats):
-        ts(("CMP", PITCH * b, PITCH * b + 128), ("BB", 0, 128), ("A16", 16 * b + 15, 16 * b + 16), beats)
-
-    def places(beats, made=0, last=2):
-        for b in range(made, 8):
-            compare(b, beats)
-        k = 8 - last
-        for b in range(k):
-            accum(("CMP", PITCH * b, PITCH * b + 129), ("PA", b, b + 1))
-        for b in range(k, 8):
-            y, p = PITCH * b, 65 * (b - k)
-            scan(("PS", p, p + 65), ("CMP", y, y + 65), ("CMP", y + 65, y + 130), 0.0, A.add, A.add)
-        copy(("PAU", k, 8), ("PS", 64, 65 * last, 65))
-        copy(("PAU", 0, k), ("PA", 0, k))
+    pick_columns(own, window("X", 0, 256), ("NN", 0, 8))
 
     mate = rank ^ 1
     exchange(mate, own, own, "arr1")
     arrive(got, "arr1")
-    hold("g", [mine], [])
-    four = [(rank ^ d, ap((name,) + mine[1:])) for d, name in ((1, "NN"), (2, "ON"), (3, "ON"))]
-    ids = [topo.addr(T.cores[m], core) for m, _ in four]
-    g.remote_dma_fused([RemoteDMATransfer(dst_ids=[DstId(rid=rid, pnc=pid) for rid, pid in ids], dma_engine_mask=topo.mask(core, T.cores[mate]),
-                                          remote_sem=T.sem["num1"], src=ap(mine), dsts=[d for _, d in four])], local_sem=T.sem["loc"])
-    sent(mate, "num1", 3)
-    arrive([theirs, ("ON", 0, 16)], "num1")
     mm(("BA", 0, 128), *U, *own)
-    scopy(("SW1", a, a + 128), ("BA", 0, 128))
-    ts(("BASE", 0, 128), ("J128", 0, 128), a + 1.0, A.add)
-    fill(("E1", 0, 256), 4096.0 if high else -4096.0)
-    fill(("CMP", 129, 8 * PITCH, PITCH), 0.0)
-    scores16(("SW1", a, a + 128))
-    iota(("I16", 0, 8), [[16, 8]], 0, 0)
-    iota(("I16R", 0, 8), [[-16, 8]], 127, 0)
-    iota(("J256", 0, 256), [[1, 256]], 0, 0)
-    ts(("CMP", 128, 8 * PITCH, PITCH), ("I16R" if high else "I16", 0, 8), ("MF", 0, 1), A.subtract if high else A.add)
+    iota(("CB", 0, 128), [[-32 if high else 32, 4], [0, 32]], 128 if high else 1, 0)
+    iota(("VC", 0, 128), [[256, 128]], 256 * (ZC + 1) - 1, 0)
+    iota(("CT", 256, 1280), [[0, 4], [1, 256]], 0, 0)
     for o in range(O):
         hold("y", [("XQ", 0, 256)], [])
         load("y", ("WT", 512 * o, 512 * o + 512), T.w[:, 512 * o:512 * o + 512], "dw%d" % o)
-    fill(("E2", 0, 256), -4096.0)
-    ts(("OWNV", 0, 128), ("J128", 0, 128), 129.0, A.add)
-    for half in (0, 128):
-        up = 1 - half // 128
-        fill(("R1", half, half + 128), float((rank & ~1) + up))
-        fill(("RO", half, half + 128), float(((rank ^ 2) & ~1) + up))
-    ts(("C1", a, a + 128), ("INV", best, best + 128), 1.0, A.subtract)
-    beats = A.is_ge if high else A.is_gt
+    half = OTH // 2
+    vpick(("EX0", 0, half), ("SCR", 0, 16), ("GOFF", 0, half // 16))
+    spick(("EX0", half, OTH), ("SCR", 0, 16), ("GOFF", half // 16, OTH // 16))
+    turn(("ST", 0, 128), ("BA", 0, 128))
+    turn(("EX", 0, half), ("EX0", 0, half))
+    turn(("EX", half, OTH), ("EX0", half, OTH))
+    scopy(("SW", 0, 128), ("BA", 0, 128))
+    low = 64 * rank
+    for c in range(4):
+        s = ("ST", 32 * c, 32 * c + 1)
+        if low:
+            ts(("CM", OTH * c, OTH * c + low), ("EX", 0, low), s, A.is_ge)
+        if low < OTH:
+            ts(("CM", OTH * c + low, OTH * c + OTH), ("EX", low, OTH), s, A.is_gt)
+        accum(("CM", OTH * c, OTH * c + OTH), ("PG", c, c + 1))
+    ts(("KCB", 0, 128), ("CB", 0, 128), ("PM", 0, 1), A.subtract if high else A.add)
+    tt(("VAL", 0, 128), ("VC", 0, 128), ("INV", best, best + 128), A.add)
+    fill(("E1", 0, 256), 256.0)
+    ts(("BASE", 0, 128), ("J128", 0, 128), a + 1.0, A.add)
+    ts(("K128", 0, 4), ("KCB", 0, 128, 32), 128.0, A.add)
+    copy(quad("X1", 0, 4, 0, 64), quad("PG", 0, 4, 64, 64))
+    scopy(quad("X1", 0, 4, 64, 64), quad("PG", 0, 4, 0, 64))
     mm(("BB", 0, 128), *U, *got)
-    tt(("G", 0, 128), ("BB", 0, 128), ("SW1", a, a + 128), beats)
-    compare(0, beats)
+    tt(("P2", 0, 4), ("PG", 0, 4), ("X1", 0, 4), A.add)
+    tt(("G", 0, 128), ("BB", 0, 128), ("SW", 0, 128), A.is_ge if high else A.is_gt)
+    for i in range(4):
+        (copy if i < 2 else scopy)(quad("X2", 0, 4, 32 * i), quad("P2", 0, 4, 32 * (i ^ 1)))
     ts(("GX", 0, 128), ("G", 0, 128), 128.0 if high else -128.0, A.mult)
-    compare(1, beats)
+    tt(("P3", 0, 4), ("P2", 0, 4), ("X2", 0, 4), A.add)
     tt(("FX", 0, 128), ("BASE", 0, 128), ("GX", 0, 128), A.add)
-    compare(2, beats)
-    off16("LOF", 0, "FH", ("FX", 0, 128), 128, lambda: compare(3, beats))
-    compare(4, beats)
-    pick_columns(window("S2", 0, 128), window("W1", 0, 256), ("LOF", 0, 8))
+    for c in range(4):
+        b = (32 * c, 32 * c + 32)
+        ts2(("BXG",) + b, ("KCB",) + b, ("P3", c, c + 1), ("K128", c, c + 1), A.add, A.min)
+    hold16(("FH", 0, 128), ("FX", 0, 128))
+    turn(("GFX", 0, 128), ("BXG", 0, 128))
+    take16(("LOF", 0, 8), ("FH", 0, 128), 1.0)
+    hold16(("GH", 0, 128), ("GFX", 0, 128))
+    S2, L2 = window("Z", ZC, ZC + 128), window("Z", ZC + 128, ZC + 256)
+    pick_columns(S2, window("W1", 0, 256), ("LOF", 0, 8))
+    take16(("LUG", 0, 8), ("GH", 0, 128), 1.0)
     mate = rank ^ 2
-    exchange(mate, window("L2", 0, 128), window("S2", 0, 128), "arr2")
-    arrive(window("L2", 0, 128), "arr2")
-    places(beats, 5, 4)
-    scopy(("SW1", z, z + 128), ("BB", 0, 128))
-    vput(("E1", 0, 256), ("PAU", 0, 8), ("BASE", 0, 128))
-    pole = A.min if high else A.max
-    scan(("TS", 0, 128), ("E1", 0, 128), ("E1", 0, 128), 129.0 if high else 128.0, pole, pole)
-    tt(("UU", 0, 128), ("TS", 0, 128), ("J128", 0, 128), A.add if high else A.subtract)
-    tt(("MX", 0, 128), ("UU", 0, 128), ("E1", 0, 128), pole)
-    off16("PU", 128, "NX", ("MX", 0, 128), 128)
-    lo1 = ("PU", 8, 16)
-    spick(("AFS", 0, 128), ("SW1", 0, 256), lo1)
-    ts2(("PI", 0, 8), ("NX", 143, 256, 16), ("SC", 0, 1), 1.0, A.mult, A.subtract)
-    if high:
-        ts(("CMP", 128, 8 * PITCH, PITCH), ("I16", 0, 8), ("MF", 0, 1), A.add)
-    ts(("PJ", 0, 8), ("PI", 0, 8), 127, A.bitwise_and)
-    copy(("PU", 0, 8), ("PJ", 0, 8))
-    send(mate, ("OP", 0, 16), ("PU", 0, 16), "num2")
-    arrive([("OP", 0, 16)], "num2")
-    scores16(("AFS", 0, 128))
-    spick(("C1", z, z + 128), ("J256", 0, 256), theirs)
-    for half in (0, 128):
-        spick(("CO", half, half + 128), ("J256", 0, 256), ("ON", half // 16, half // 16 + 8))
-    spick(("R2", 128, 256), ("R1", 0, 256), lo1)
-    spick(("C2", 128, 256), ("C1", 0, 256), lo1)
-
-    for h in (2, 3):
-        w, c, r = "W%d" % h, "C%d" % h, "R%d" % h
-        own = window(w, 128, 256)
-        if h == 3:
-            mate = rank ^ 4
-            got = window(w, 0, 128)
-            exchange(mate, got, own, "arr3")
-            arrive(got, "arr3")
-            mm(("BA", 0, 128), *U, *own)
-            fill(("E3", 0, 256), -4096.0)
-            for o in range(O):
-                quant(("WQ", 128 * o, 128 * o + 128), ("WS", 128 * o, 128 * o + 128), ("WT", 512 * o, 512 * o + 512))
-            scores16(("BA", 0, 128))
-            lists = [((128 * i, 128 * i + 128), b) for i, b in enumerate((r, c))]
-            for at, b in lists:
-                tt(("NX",) + at, (b, 128, 256), ("MASK", 0, 128), A.mult)
-            for at, b in lists:
-                scan(("NH",) + at, ("HOLD", 0, 128), ("NX",) + at, 0.0, A.mult, A.add)
-            for at, b in lists:
-                copy(("NS3", at[0] // 16, at[1] // 16), ("NH", at[0] + 15, at[1], 16))
-            send(mate, ("NL3", 0, 16), ("NS3", 0, 16), "num3")
-            arrive([("NL3", 0, 16)], "num3")
-            for o in range(O):
-                mm(("BY%d" % o, 0, 128), *window("W", 128 * o, 128 * o + 128), *own)
-                scopy(("RES%d" % o, 128, 256), ("BY%d" % o, 0, 128))
-        else:
-            got = window("L2", 0, 128)
-        mm(("BB", 0, 128), *U, *got)
-        if h == 3:
-            for o in range(O):
-                mm(("BS%d" % o, 0, 128), *window("W", 128 * o, 128 * o + 128), *got)
-        places(A.is_ge if rank >> (h - 1) & 1 else A.is_gt)
-        e, lo = ("E%d" % h, 0, 128), ("LO%d" % h, 0, 8)
-        vput((e[0], 0, 256), ("PAU", 0, 8), ("OWNV", 0, 128))
-        if h == 2:
-            pick_columns(own, window("W1", 0, 256), lo1)
-        scan(("TS", 0, 128), e, e, 128.0, A.max, A.max)
-        tt(("UU", 0, 128), ("OWNV", 0, 128), ("TS", 0, 128), A.subtract)
-        tt(("MX", 0, 128), ("UU", 0, 128), e, A.max)
-        if h == 2:
-            pick_columns(window(w, 0, 128), got, ("OP", 0, 8))
-        off16("LO%d" % h, 0, "MH", ("MX", 0, 128), 128)
-        if h == 2:
-            pick_columns(window("W3", 128, 256), window(w, 0, 256), lo)
-            spick((r, 0, 128), ("RO", 0, 256), ("OP", 8, 16))
-            spick((c, 0, 128), ("CO", 0, 256), ("OP", 8, 16))
-            spick(("R3", 128, 256), (r, 0, 256), lo)
-            spick(("C3", 128, 256), (c, 0, 256), lo)
-        else:
-            for o in range(O):
-                scopy(("RES%d" % o, 0, 128), ("BS%d" % o, 0, 128))
-            spick((r, 0, 128), ("J256", 0, 256), ("NL3", 0, 8))
-            spick((c, 0, 128), ("J256", 0, 256), ("NL3", 8, 16))
-            vpick(("YB", 0, 128), ("RES0", 0, 256), lo)
-            spick(("YB", 128, 256), ("RES1", 0, 256), lo)
-            do("y", lambda: g.sync.dma_start(T.y[:, :], ap(("YB", 0, 256))), [], [("YB", 0, 256)], "dy", 16)
-            vpick(("IDB", 0, 128), (r, 0, 256), lo)
-            spick(("IDB", 128, 256), (c, 0, 256), lo)
-            do("s", lambda: g.scalar.dma_start(T.id[:, :], T.IDB[0:1, 0:256]), [], [("IDB", 0, 256)], "did", 16)
+    exchange(mate, L2, S2, "arr2")
+    arrive(L2, "arr2")
+    vput(("E1", 0, 256), ("LUG", 0, 8), ("VAL", 0, 128))
+    hold16(("EH", 0, 128), ("E1", 0, 128))
+    take16(("LV4", 0, 8), ("EH", 0, 128), 256.0)
+    place = {0: 0, 2: 8, 1: 16, 3: 24}
+    spread([rank ^ d for d in (1, 2, 3)], [("LV4", place[d], place[d] + 8) for d in (1, 2, 3)], ("LV4", 0, 8), "num1")
+    arrive([("LV4", 8, 32)], "num1")
+    fill(("ZOFF", 0, 2), 256)
+    pick_columns(window("Z", 0, ZC), window("X", 0, 256 + ZC), ("ZOFF", 0, 1))
+    for o in range(O):
+        quant(("WQ", 128 * o, 128 * o + 128), ("WS", 128 * o, 128 * o + 128), ("WT", 512 * o, 512 * o + 512))
+    fill(("CT", 0, 256), 0.0)
+    for name, first in (("RTO", rank & 4), ("RTA", rank & 4 ^ 4)):
+        fill((name, 0, 256), 0.0)
+        for i in range(4):
+            fill((name, 256 * i + 256, 256 * i + 512), float(first + i))
+    copy(("VI", 0, 32), ("LV4", 0, 32))
+    tt(("MO", 0, 16), ("VI", 0, 16), ("VI", 16, 32), A.max)
+    ts(("AN", 0, 32), ("VI", 0, 32), 255, A.bitwise_and)
+    ts2(("FO", 0, 8), ("MO", 8, 16), 0.0, 256.0 * 128, A.is_gt, A.mult)
+    tt(("TM", 0, 8), ("MO", 0, 8), ("MO", 8, 16), A.add)
+    for d in (0, 1):
+        ts2(("GN", place[d], place[d] + 8), ("VI", place[d], place[d] + 8), 0.0, 256.0 * (((rank ^ d) & 3) + 1), A.is_gt, A.mult)
+    tt(("TC", 0, 8), ("TM", 0, 8), ("FO", 0, 8), A.add)
+    for d in (2, 3):
+        ts2(("GN", place[d], place[d] + 8), ("VI", place[d], place[d] + 8), 0.0, 256.0 * (((rank ^ d) & 3) + 1), A.is_gt, A.mult)
+    ts(("TK", 0, 8), ("TC", 0, 8), 8, A.arith_shift_right)
+    tt(("SN", 0, 32), ("AN", 0, 32), ("GN", 0, 32), A.add)
+    copy(("LC", 0, 8), ("TK", 0, 8))
+    tt(("SM", 0, 16), ("SN", 0, 16), ("SN", 16, 32), A.add)
+    V4, L4 = window("V4", 0, 128), window("L4", 0, 128)
+    pick_columns(V4, window("Z", 0, 256 + ZC), ("LC", 0, 8))
+    mate = rank ^ 4
+    exchange(mate, L4, V4, "arr3")
+    arrive(L4, "arr3")
+    tt(("NI", 0, 8), ("SM", 0, 8), ("SM", 8, 16), A.add)
+    copy(("LID", 0, 8), ("NI", 0, 8))
+    send(mate, ("LIA", 0, 8), ("LID", 0, 8), "num3")
+    arrive([("LIA", 0, 8)], "num3")
+    for o in range(O):
+        mm(("BY%d" % o, 0, 128), *window("W", 128 * o, 128 * o + 128), *V4, True, False)
+    vpick(("IDO", 0, 128), ("RTO", 0, 1280), ("LID", 0, 8))
+    spick(("IDO", 128, 256), ("CT", 0, 1280), ("LID", 0, 8))
+    for o in range(O):
+        mm(("BY%d" % o, 0, 128), *window("W", 128 * o, 128 * o + 128), *L4, False, True)
+    copy(("YB", 0, 128), ("BY0", 0, 128))
+    scopy(("YB", 128, 256), ("BY1", 0, 128))
+    do("y", lambda: g.sync.dma_start(T.y[:, :], ap(("YB", 0, 256))), [], [("YB", 0, 256)], "dy", 16)
+    vpick(("IDA", 0, 128), ("RTA", 0, 1280), ("LIA", 0, 8))
+    spick(("IDA", 128, 256), ("CT", 0, 1280), ("LIA", 0, 8))
+    tt(("IDB", 0, 256), ("IDO", 0, 256), ("IDA", 0, 256), A.add)
+    do("s", lambda: g.scalar.dma_start(T.id[:, :], T.IDB[0:1, 0:256]), [], [("IDB", 0, 256)], "did", 16)
     late = ("t", "v", "s", "did", "dy")
     for sem in sorted(x for x in total if x not in late) + list(late):
         if known["g"].get(sem, 0) < total[sem]:

from concourse.bass import DstId, RemoteDMATransfer
from concourse.mybir import dt, AluOpType, ActivationFunctionType

N, T_COLS, K, O = 8, 256, 128, 2
BF, F32, U16, I32, CODE, U8 = "bfloat16", "float32", "uint16", "int32", "float8_e4m3fn_x4", "uint8"
OTH = 64 * (N - 1)
ZC = 16


def _sbuf(cols, dtype, names):
    return {n: ("sbuf", [128, cols], dtype) for n in names.split()}


SCRATCH = {}
SCRATCH.update(_sbuf(512, BF, "UT"))
SCRATCH.update(_sbuf(1024 + 4 * ZC, BF, "XT"))
SCRATCH.update(_sbuf(1024, BF, "WT"))
SCRATCH.update(_sbuf(128, CODE, "UQ0 UQ V4Q L4Q"))
SCRATCH.update(_sbuf(128, U8, "US0 US V4S L4S"))
SCRATCH.update(_sbuf(256, CODE, "WQ W1Q"))
SCRATCH.update(_sbuf(256, U8, "WS W1S"))
SCRATCH.update(_sbuf(256 + ZC, CODE, "XQ ZQ"))
SCRATCH.update(_sbuf(256 + ZC, U8, "XS ZS"))
SCRATCH.update(_sbuf(8, U16, "UOFF NN LOF LUG LC LID LIA"))
SCRATCH.update(_sbuf(2, U16, "ZOFF"))
SCRATCH.update(_sbuf(16, U16, "LU"))
SCRATCH.update(_sbuf(32, U16, "LV4"))
SCRATCH.update(_sbuf(4 * (N - 1), U16, "GOFF"))
SCRATCH.update(_sbuf(4 * (N - 1), BF, "GO"))
SCRATCH.update(_sbuf(1, I32, "PIDX MI MJ"))
SCRATCH.update(_sbuf(8, I32, "FO TM TC TK NI"))
SCRATCH.update(_sbuf(16, I32, "MO SM"))
SCRATCH.update(_sbuf(32, I32, "VI AN GN SN"))
SCRATCH.update(_sbuf(1, F32, "MF PF MF1 SC0 SC LR PM"))
SCRATCH.update(_sbuf(2, F32, "SCO"))
SCRATCH.update(_sbuf(16, F32, "SCR"))
SCRATCH.update(_sbuf(4, F32, "PG X1 P2 X2 P3 K128"))
SCRATCH.update(_sbuf(256, BF, "JC TRI EQ LRF LH INV IDO IDA"))
SCRATCH.update(_sbuf(128, BF, "J128 TMOD HOLD HE HB BASE ZB G GX FX FH NH CB KCB BXG GFX GH"))
SCRATCH.update(_sbuf(1280, BF, "RTO RTA CT"))
SCRATCH.update(_sbuf(768, BF, "CH"))
SCRATCH.update(_sbuf(192, BF, "LS"))
SCRATCH.update(_sbuf(64, BF, "BX"))
SCRATCH.update(_sbuf(4 * OTH, BF, "CM"))
SCRATCH.update(_sbuf(OTH, F32, "EX0 EX"))
SCRATCH.update(_sbuf(128, F32, "ST SW VC VAL EH"))
SCRATCH.update(_sbuf(256, F32, "E1 YB IDB"))
PSUM_NAMES = ["BSF", "BS0", "BS1", "BA", "BB", "BY0", "BY1"]
SCRATCH.update({n: ("psum", [128, 512], F32) for n in PSUM_NAMES})
SEMAPHORES = ["v", "s", "t", "gc", "du", "dx0", "dx1", "dw0", "dw1", "dy", "did", "loc",
              "arr1", "arr2", "arr3", "sc", "num1", "num3"]


def rank_program(g, core, T, topo):
    rank = T.rank_of(core)
    if rank is None:
        return
    A = AluOpType
    F = ActivationFunctionType
    engines = {"v": g.vector, "s": g.scalar, "t": g.tensor, "g": g, "y": g.sync}
    known = {q: {} for q in engines}
    total = {}
    hist = {}

    def parts(r):
        return (r[4], r[5]) if len(r) > 4 else (0, 128)

    def record(reads, writes, q, sem, val, clock):
        for rs, w in ((reads, False), (writes, True)):
            for r in rs:
                hist.setdefault(r[0], []).append((r[1], r[2]) + parts(r) + (w, q, sem, val, clock))

    def hold(q, reads, writes):
        need = {}
        for rs, w in ((reads, False), (writes, True)):
            for r in rs:
                psum = r[0] in PSUM_NAMES
                a, z = parts(r)
                for lo, hi, p0, p1, hw, hq, sem, val, clock in hist.get(r[0], []):
                    if not (psum or (lo < r[2] and r[1] < hi and p0 < z and a < p1)):
                        continue
                    if not (w or hw or (psum and hq != q)):
                        continue
                    if known[q].get(sem, 0) < val and (sem not in need or need[sem][0] < val):
                        need[sem] = (val, clock)
        for sem in sorted(need):
            val, clock = need[sem]
            if any(o != sem and need[o][1].get(sem, 0) >= val for o in need):
                continue
            engines[q].wait_ge(T.sem[sem], val)
        for sem in need:
            val, clock = need[sem]
            for s, x in list(clock.items()) + [(sem, val)]:
                known[q][s] = max(known[q].get(s, 0), x)

    def do(q, call, writes, reads, sem=None, inc=1):
        sem = sem or {"g": "gc"}.get(q, q)
        hold(q, reads, writes)
        call().then_inc(T.sem[sem], inc)
        total[sem] = total.get(sem, 0) + inc
        clock = dict(known[q])
        clock[sem] = total[sem]
        record(reads, writes, q, sem, total[sem], clock)

    def ap(r):
        if len(r) == 3:
            return T[r[0]][:, r[1]:r[2]]
        p, z = parts(r)
        return T[r[0]][p:z, r[1]:r[2]:r[3]]

    def words(r):
        return ap(r).bitcast(dt.uint32)

    def ts2(out, in0, s, s2, op0, op1):
        cols = [x for x in (s, s2) if isinstance(x, tuple)]
        a, b = [ap(x) if isinstance(x, tuple) else x for x in (s, s2)]
        last = () if op1 is None else (op1,)
        do("v", lambda: g.vector.tensor_scalar(ap(out), ap(in0), a, b, op0, *last), [out], [in0] + cols)

    def ts(out, in0, s, op):
        ts2(out, in0, s, None, op, None)

    def tt(out, a, b, op):
        do("v", lambda: g.vector.tensor_tensor(ap(out), ap(a), ap(b), op), [out], [a, b])

    def scan(out, a, b, init, op0, op1):
        do("v", lambda: g.vector.tensor_tensor_scan(ap(out), ap(a), ap(b), init, op0, op1), [out], [a, b])

    def turn(out, a):
        do("v", lambda: g.vector.transpose(ap(out), ap(a)), [out], [a])

    def copy(out, a):
        do("v", lambda: g.vector.tensor_copy(ap(out), ap(a)), [out], [a])

    def scopy(out, a):
        do("s", lambda: g.scalar.activation(ap(out), ap(a), F.Copy), [out], [a])

    def vpick(out, win, off):
        do("v", lambda: g.vector.tensor_copy(ap(out), ap(win).indirect(ap(off))), [out], [win, off])

    def vput(win, off, src):
        do("v", lambda: g.vector.tensor_copy(ap(win).indirect(ap(off)), ap(src)), [win], [off, src])

    def spick(out, win, off):
        do("s", lambda: g.scalar.activation(ap(out), ap(win).indirect(ap(off)), F.Copy), [out], [win, off])

    def pick_columns(out, win, off):
        do("v", lambda: g.vector.tensor_copy(words(out[0]), words(win[0]).indirect(ap(off))), [out[0]], [win[0], off])
        spick(out[1], win[1], off)

    def fill(out, x):
        do("v", lambda: g.vector.memset(ap(out), x), [out], [])

    def iota(out, pattern, base, cm):
        do("g", lambda: g.iota(ap(out), pattern, base, cm, allow_small_or_imprecise_dtypes=True), [out], [])

    def quant(q, s, t):
        do("v", lambda: g.vector.quantize_mx(ap(q), ap(s), ap(t)), [q, s], [t])

    def mm(out, wq, ws, xq, xs, start=True, stop=True):
        do("t", lambda: g.tensor.matmul_mx(ap(out), ap(wq), ap(ws), ap(xq), ap(xs), start, stop), [out], [wq, ws, xq, xs])

    def accum(buf, out):
        do("s", lambda: g.scalar.activation(ap(buf), ap(buf), F.Identity, accum_out=ap(out)), [buf, out], [buf])

    def hold16(tmp, x):
        scan(tmp, ("HB", 0, tmp[2] - tmp[1]), x, 0.0, A.mult, A.max)

    def take16(out, tmp, less):
        ts2(out, (tmp[0], tmp[1] + 15, tmp[2], 16), ("SC", 0, 1), less, A.mult, A.subtract)

    def load(q, out, src, sem):
        do(q, lambda: engines[q].dma_start(ap(out), src), [out], [], sem, 16)

    def sent(mate, rsem, copies=1):
        n = len(topo.engines(core, T.cores[mate]))
        total["loc"] = total.get("loc", 0) + n
        total[rsem] = total.get(rsem, 0) + n * copies

    def send(mate, out, src, rsem, codes=False):
        dst = T.cores[mate]
        hold("g", [src], [])
        rid, pid = topo.addr(dst, core)
        a, b = (ap(out).bitcast(dt.uint8), ap(src).bitcast(dt.uint8)) if codes else (ap(out), ap(src))
        g.remote_dma(a, b, T.sem[rsem], T.sem["loc"], pid, rid, topo.mask(core, dst))
        sent(mate, rsem)

    def spread(mates, outs, src, rsem):
        hold("g", [src], [])
        ids = [topo.addr(T.cores[m], core) for m in mates]
        g.remote_dma_fused([RemoteDMATransfer(
            dst_ids=[DstId(rid=rid, pnc=pid) for rid, pid in ids], dma_engine_mask=topo.mask(core, T.cores[mates[0]]),
            remote_sem=T.sem[rsem], src=ap(src), dsts=[ap(o) for o in outs])], local_sem=T.sem["loc"])
        sent(mates[0], rsem, len(mates))

    def arrive(regions, sem):
        record([], regions, "-", sem, total[sem], {sem: total[sem]})

    def exchange(mate, out, src, sem):
        send(mate, out[0], src[0], sem, codes=True)
        send(mate, out[1], src[1], sem)

    def window(name, a, b):
        return (name + "Q", a, b), (name + "S", a, b)

    high = rank & 1

    load("y", ("UT", 0, 8), T.u[:, 0:8], "du")
    load("s", ("XT", 0, 512), T.x[:, 0:512], "dx0")
    load("y", ("XT", 512, 1024), T.x[:, 512:1024], "dx1")

    fill(("UT", 8, 512), 0.0)
    fill(("XT", 1024, 1024 + 4 * ZC), 0.0)
    fill(("UOFF", 0, 8), 0)
    iota(("PIDX", 0, 1), [[0, 1]], 0, 1)
    iota(("J128", 0, 128), [[1, 128]], 0, 0)
    iota(("TMOD", 0, 128), [[0, 8], [1, 16]], 0, 0)
    iota(("JC", 0, 256), [[32, 4], [128, 2], [1, 32]], 1, 0)
    if rank:
        iota(("GO", 0, 4 * rank), [[1, 2 * rank], [0, 2]], 0, 0)
    if rank < N - 1:
        iota(("GO", 4 * rank, 4 * (N - 1)), [[1, 2 * (N - 1 - rank)], [0, 2]], 2 * rank + 2, 0)
    ts(("MI", 0, 1), ("PIDX", 0, 1), 15, A.bitwise_and)
    ts(("MJ", 0, 1), ("PIDX", 0, 1), 31, A.bitwise_and)
    copy(("PF", 0, 1), ("PIDX", 0, 1))
    copy(("MF", 0, 1), ("MI", 0, 1))
    copy(("PM", 0, 1), ("MJ", 0, 1))
    for h in (0, 1):
        ts(("TRI", 128 * h, 128 * h + 128), ("J128", 0, 128), ("PF", 0, 1), A.is_lt)

    quant(("UQ0", 0, 128), ("US0", 0, 128), ("UT", 0, 512))
    U = (("UQ", 0, 128), ("US", 0, 128))
    pick_columns(U, (("UQ0", 0, 128), ("US0", 0, 128)), ("UOFF", 0, 8))
    quant(("XQ", 0, 128), ("XS", 0, 128), ("XT", 0, 512))
    quant(("XQ", 128, 256 + ZC), ("XS", 128, 256 + ZC), ("XT", 512, 1024 + 4 * ZC))
    for h in (0, 1):
        mm(("BY%d" % h, 0, 128), *window("X", 128 * h, 128 * h + 128), *U)
        scopy(("SCO", h, h + 1), ("BY%d" % h, 0, 1))
        if h == 0:
            mm(("BS0", 0, 128), *window("X", 0, 128), *U)
            mm(("BSF", 0, 256), *U, *window("X", 0, 256))
    mm(("BS1", 0, 128), *window("X", 128, 256), *U)
    others = [s for s in range(N) if s != rank]
    spread(others, [("SCR", 2 * rank, 2 * rank + 2)] * (N - 1), ("SCO", 0, 2), "sc")
    arrive([("SCR", 0, 16)], "sc")
    fill(("ZB", 0, 128), 0.0)
    ts(("MF1", 0, 1), ("MF", 0, 1), 1.0, A.add)
    ts2(("SC0", 0, 1), ("MF", 0, 1), 15.0, 255.0 / 256.0, A.is_equal, A.mult)
    ts(("HOLD", 0, 128), ("TMOD", 0, 128), ("MF", 0, 1), A.is_gt)
    ts2(("HE", 0, 128), ("TMOD", 0, 128), ("MF1", 0, 1), 255.0, A.is_equal, A.mult)
    ts(("SC", 0, 1), ("SC0", 0, 1), 1.0 / 256.0, A.add)

    s0, s1 = ("BS0", 0, 1), ("BS1", 0, 1)
    ts(("EQ", 0, 128), ("BSF", 0, 128), s0, A.is_equal)
    ts(("EQ", 128, 256), ("BSF", 128, 256), s1, A.is_equal)
    ts(("CH", 0, 256), ("BSF", 0, 256), s0, A.is_gt)
    tt(("CH", 256, 512), ("EQ", 0, 256), ("TRI", 0, 256), A.mult)
    accum(("CH", 0, 384), ("LR", 0, 1))
    ts(("CH", 512, 640), ("BSF", 0, 128), s1, A.is_ge)
    ts(("CH", 640, 768), ("BSF", 128, 256), s1, A.is_gt)
    tt(("HB", 0, 128), ("HOLD", 0, 128), ("HE", 0, 128), A.add)
    scan(("LS", 0, 192), ("CH", 384, 576), ("CH", 576, 768), 0.0, A.add, A.add)
    copy(("GOFF", 0, 4 * (N - 1)), ("GO", 0, 4 * (N - 1)))
    for h, col in ((0, ("LR", 0, 1)), (1, ("LS", 191, 192))):
        ts2(("BX", 32 * h, 32 * h + 32), ("ZB", 0, 32), col, 256.0 if high else 1.0, A.subtract if high else A.add, A.add)

    def quad(name, a, b, p, n=32):
        return (name, a, b, 1, p, p + n)

    for a in range(4):
        turn(quad("LRF", 64 * a, 64 * a + 64, 32 * a), quad("BX", 0, 64, 32 * a))
    for a in range(4):
        c = (64 * a, 64 * a + 64)
        (copy if a < 2 else scopy)(quad("LRF", *c, 32 * (a ^ 1)), quad("LRF", *c, 32 * a))
    copy(quad("LRF", 0, 128, 64, 64), quad("LRF", 0, 128, 0, 64))
    scopy(quad("LRF", 128, 256, 0, 64), quad("LRF", 128, 256, 64, 64))
    for a in (0, 128):
        hold16(("LH", a, a + 128), ("LRF", a, a + 128))
    for a in (0, 128):
        take16(("LU", a // 16, a // 16 + 8), ("LH", a, a + 128), 1.0)
    vput(("INV", 0, 256), ("LU", 0, 16), ("JC", 0, 256))
    best = 128 if high else 0
    a, z = (0, 128) if high else (128, 0)
    hold16(("NH", 0, 128), ("INV", best, best + 128))
    take16(("NN", 0, 8), ("NH", 0, 128), 1.0)
    own, got = window("W1", a, a + 128), window("W1", z, z + 128)
    pick_columns(own, window("X", 0, 256), ("NN", 0, 8))

    mate = rank ^ 1
    exchange(mate, own, own, "arr1")
    arrive(got, "arr1")
    mm(("BA", 0, 128), *U, *own)
    iota(("CB", 0, 128), [[-32 if high else 32, 4], [0, 32]], 128 if high else 1, 0)
    iota(("VC", 0, 128), [[256, 128]], 256 * (ZC + 1) - 1, 0)
    iota(("CT", 256, 1280), [[0, 4], [1, 256]], 0, 0)
    for o in range(O):
        hold("y", [("XQ", 0, 256)], [])
        load("y", ("WT", 512 * o, 512 * o + 512), T.w[:, 512 * o:512 * o + 512], "dw%d" % o)
    half = OTH // 2
    vpick(("EX0", 0, half), ("SCR", 0, 16), ("GOFF", 0, half // 16))
    spick(("EX0", half, OTH), ("SCR", 0, 16), ("GOFF", half // 16, OTH // 16))
    turn(("ST", 0, 128), ("BA", 0, 128))
    turn(("EX", 0, half), ("EX0", 0, half))
    turn(("EX", half, OTH), ("EX0", half, OTH))
    scopy(("SW", 0, 128), ("BA", 0, 128))
    low = 64 * rank
    for c in range(4):
        s = ("ST", 32 * c, 32 * c + 1)
        if low:
            ts(("CM", OTH * c, OTH * c + low), ("EX", 0, low), s, A.is_ge)
        if low < OTH:
            ts(("CM", OTH * c + low, OTH * c + OTH), ("EX", low, OTH), s, A.is_gt)
        accum(("CM", OTH * c, OTH * c + OTH), ("PG", c, c + 1))
    ts(("KCB", 0, 128), ("CB", 0, 128), ("PM", 0, 1), A.subtract if high else A.add)
    tt(("VAL", 0, 128), ("VC", 0, 128), ("INV", best, best + 128), A.add)
    fill(("E1", 0, 256), 256.0)
    ts(("BASE", 0, 128), ("J128", 0, 128), a + 1.0, A.add)
    ts(("K128", 0, 4), ("KCB", 0, 128, 32), 128.0, A.add)
    copy(quad("X1", 0, 4, 0, 64), quad("PG", 0, 4, 64, 64))
    scopy(quad("X1", 0, 4, 64, 64), quad("PG", 0, 4, 0, 64))
    mm(("BB", 0, 128), *U, *got)
    tt(("P2", 0, 4), ("PG", 0, 4), ("X1", 0, 4), A.add)
    tt(("G", 0, 128), ("BB", 0, 128), ("SW", 0, 128), A.is_ge if high else A.is_gt)
    for i in range(4):
        (copy if i < 2 else scopy)(quad("X2", 0, 4, 32 * i), quad("P2", 0, 4, 32 * (i ^ 1)))
    ts(("GX", 0, 128), ("G", 0, 128), 128.0 if high else -128.0, A.mult)
    tt(("P3", 0, 4), ("P2", 0, 4), ("X2", 0, 4), A.add)
    tt(("FX", 0, 128), ("BASE", 0, 128), ("GX", 0, 128), A.add)
    for c in range(4):
        b = (32 * c, 32 * c + 32)
        ts2(("BXG",) + b, ("KCB",) + b, ("P3", c, c + 1), ("K128", c, c + 1), A.add, A.min)
    hold16(("FH", 0, 128), ("FX", 0, 128))
    turn(("GFX", 0, 128), ("BXG", 0, 128))
    take16(("LOF", 0, 8), ("FH", 0, 128), 1.0)
    hold16(("GH", 0, 128), ("GFX", 0, 128))
    S2, L2 = window("Z", ZC, ZC + 128), window("Z", ZC + 128, ZC + 256)
    pick_columns(S2, window("W1", 0, 256), ("LOF", 0, 8))
    take16(("LUG", 0, 8), ("GH", 0, 128), 1.0)
    mate = rank ^ 2
    exchange(mate, L2, S2, "arr2")
    arrive(L2, "arr2")
    vput(("E1", 0, 256), ("LUG", 0, 8), ("VAL", 0, 128))
    hold16(("EH", 0, 128), ("E1", 0, 128))
    take16(("LV4", 0, 8), ("EH", 0, 128), 256.0)
    place = {0: 0, 2: 8, 1: 16, 3: 24}
    spread([rank ^ d for d in (1, 2, 3)], [("LV4", place[d], place[d] + 8) for d in (1, 2, 3)], ("LV4", 0, 8), "num1")
    arrive([("LV4", 8, 32)], "num1")
    fill(("ZOFF", 0, 2), 256)
    pick_columns(window("Z", 0, ZC), window("X", 0, 256 + ZC), ("ZOFF", 0, 1))
    for o in range(O):
        quant(("WQ", 128 * o, 128 * o + 128), ("WS", 128 * o, 128 * o + 128), ("WT", 512 * o, 512 * o + 512))
    fill(("CT", 0, 256), 0.0)
    for name, first in (("RTO", rank & 4), ("RTA", rank & 4 ^ 4)):
        fill((name, 0, 256), 0.0)
        for i in range(4):
            fill((name, 256 * i + 256, 256 * i + 512), float(first + i))
    copy(("VI", 0, 32), ("LV4", 0, 32))
    tt(("MO", 0, 16), ("VI", 0, 16), ("VI", 16, 32), A.max)
    ts(("AN", 0, 32), ("VI", 0, 32), 255, A.bitwise_and)
    ts2(("FO", 0, 8), ("MO", 8, 16), 0.0, 256.0 * 128, A.is_gt, A.mult)
    tt(("TM", 0, 8), ("MO", 0, 8), ("MO", 8, 16), A.add)
    for d in (0, 1):
        ts2(("GN", place[d], place[d] + 8), ("VI", place[d], place[d] + 8), 0.0, 256.0 * (((rank ^ d) & 3) + 1), A.is_gt, A.mult)
    tt(("TC", 0, 8), ("TM", 0, 8), ("FO", 0, 8), A.add)
    for d in (2, 3):
        ts2(("GN", place[d], place[d] + 8), ("VI", place[d], place[d] + 8), 0.0, 256.0 * (((rank ^ d) & 3) + 1), A.is_gt, A.mult)
    ts(("TK", 0, 8), ("TC", 0, 8), 8, A.arith_shift_right)
    tt(("SN", 0, 32), ("AN", 0, 32), ("GN", 0, 32), A.add)
    copy(("LC", 0, 8), ("TK", 0, 8))
    tt(("SM", 0, 16), ("SN", 0, 16), ("SN", 16, 32), A.add)
    V4, L4 = window("V4", 0, 128), window("L4", 0, 128)
    pick_columns(V4, window("Z", 0, 256 + ZC), ("LC", 0, 8))
    mate = rank ^ 4
    exchange(mate, L4, V4, "arr3")
    arrive(L4, "arr3")
    tt(("NI", 0, 8), ("SM", 0, 8), ("SM", 8, 16), A.add)
    copy(("LID", 0, 8), ("NI", 0, 8))
    send(mate, ("LIA", 0, 8), ("LID", 0, 8), "num3")
    arrive([("LIA", 0, 8)], "num3")
    for o in range(O):
        mm(("BY%d" % o, 0, 128), *window("W", 128 * o, 128 * o + 128), *V4, True, False)
    vpick(("IDO", 0, 128), ("RTO", 0, 1280), ("LID", 0, 8))
    spick(("IDO", 128, 256), ("CT", 0, 1280), ("LID", 0, 8))
    for o in range(O):
        mm(("BY%d" % o, 0, 128), *window("W", 128 * o, 128 * o + 128), *L4, False, True)
    copy(("YB", 0, 128), ("BY0", 0, 128))
    scopy(("YB", 128, 256), ("BY1", 0, 128))
    do("y", lambda: g.sync.dma_start(T.y[:, :], ap(("YB", 0, 256))), [], [("YB", 0, 256)], "dy", 16)
    vpick(("IDA", 0, 128), ("RTA", 0, 1280), ("LIA", 0, 8))
    spick(("IDA", 128, 256), ("CT", 0, 1280), ("LIA", 0, 8))
    tt(("IDB", 0, 256), ("IDO", 0, 256), ("IDA", 0, 256), A.add)
    do("s", lambda: g.scalar.dma_start(T.id[:, :], T.IDB[0:1, 0:256]), [], [("IDB", 0, 256)], "did", 16)
    late = ("t", "v", "s", "did", "dy")
    for sem in sorted(x for x in total if x not in late) + list(late):
        if known["g"].get(sem, 0) < total[sem]:
            g.wait_ge(T.sem[sem], total[sem])
